import numpy as np
import ml_dtypes


def mxq(x, axis, fmt="e4m3"):
    dtype, down = {"e4m3": (ml_dtypes.float8_e4m3fn, 7), "e5m2": (ml_dtypes.float8_e5m2, 14)}[fmt]
    v = np.moveaxis(np.asarray(x, np.float32).astype(ml_dtypes.bfloat16).astype(np.float64), axis, -1)
    blocks = v.reshape(v.shape[:-1] + (-1, 32))
    amax = np.abs(blocks).max(-1, keepdims=True)
    byte = np.maximum(np.where(amax > 0, np.frexp(amax)[1] - 1 + 127, 0) - down, 1)
    scale = np.exp2(byte - 127.0)
    codes = (blocks / scale).astype(np.float32).astype(dtype).astype(np.float64)
    return np.moveaxis((codes * scale).reshape(v.shape), -1, axis)


WIDE = False


def mx_kscale(k):
    if not WIDE:
        return np.ones(k)
    levels = np.array([10, -10, 5, -5, 0])
    if k % 512:
        return np.exp2(np.random.permutation(np.resize(levels, k // 32))).repeat(32)
    a = np.empty((k // 512, 16))
    for p in range(k // 512):
        a[p, :8] = np.random.permutation(np.resize(levels, 8))
        for g in range(8):
            far = levels[np.abs(levels - a[p, g]) >= 10]
            a[p, g + 8] = far[np.random.randint(len(far))]
    return np.exp2(a.ravel()).repeat(32)


BF16 = ml_dtypes.bfloat16


def bf(x):
    return np.asarray(x, np.float32).astype(BF16)


def f64(x):
    return np.asarray(x).astype(np.float64)


E2M1 = np.array([0.0, 0.5, 1.0, 1.5, 2.0, 3.0, 4.0, 6.0, -0.0, -0.5, -1.0, -1.5, -2.0, -3.0, -4.0, -6.0])


def pack_weight(w, fmt):
    k, n = w.shape
    w = f64(bf(w)).reshape(k // 32, 32, n)
    amax = np.abs(w).max(1)
    if fmt == "e4m3":
        byte = np.frexp(amax)[1] - 1 + 127 - 7
    else:
        mant, ex = np.frexp(amax / 6.0)
        byte = np.where(mant > 0.5, ex, ex - 1) + 127
    byte = np.clip(np.where(amax > 0, byte, 1), 1, 254)
    scaled = (w * np.exp2(127.0 - byte)[:, None, :]).reshape(k, n).astype(np.float32)
    by_word = np.ascontiguousarray(scaled.reshape(k // 512, 128, 4, n).transpose(0, 1, 3, 2))
    if fmt == "e4m3":
        words = by_word.astype(ml_dtypes.float8_e4m3fn).view(np.uint8)
    else:
        c = by_word.astype(ml_dtypes.float4_e2m1fn).view(np.uint8) & 0xF
        words = c[..., 0::2] | (c[..., 1::2] << 4)
    return np.ascontiguousarray(words), np.ascontiguousarray(byte.astype(np.uint8).reshape(k // 512, 16, n))


def unpack_weight(words, scales, fmt):
    g, p, n, _ = words.shape
    if fmt == "e4m3":
        vals = np.ascontiguousarray(words).view(ml_dtypes.float8_e4m3fn).astype(np.float64)
    else:
        nib = np.empty((g, p, n, 4), np.uint8)
        nib[..., 0::2] = words & 0xF
        nib[..., 1::2] = words >> 4
        vals = E2M1[nib]
    vals = vals * np.repeat(np.exp2(scales.astype(np.float64) - 127.0), 8, axis=1)[..., None]
    return vals.transpose(0, 1, 3, 2).reshape(g * 512, n)
def pack4(w):
    words, scales = pack_weight(w, "e2m1")
    return words.reshape(words.shape[0], 128, -1), scales


def unpack4(words, scales):
    return unpack_weight(words.reshape(words.shape[0], 128, -1, 2), scales, "e2m1")


E4M3FN = np.array([(-1.0 if i & 128 else 1.0) * ((1.0 + (i & 7) / 8.0) * 2.0 ** (((i >> 3) & 15) - 7) if i & 120 else (i & 7) * 2.0 ** -9) for i in range(256)])


def e4m3fn_bytes(y):
    return np.clip(np.asarray(y, np.float64), -448.0, 448.0).astype(np.float32).astype(ml_dtypes.float8_e4m3fn).view(np.uint8)


def e4m3fn_values(b):
    return E4M3FN[b]


T, D, H, E, F, B = 512, 1536, 16, 128, 2048, 128


def setup_inputs():
    s, t = mx_kscale(D), mx_kscale(F)
    X = np.random.standard_normal((T, D)) * s
    Wg = 2.0 * np.random.standard_normal((D, F)) / np.sqrt(D) / s[:, None]
    X_scale = (np.abs(X).reshape(T, D // B, B).max(axis=2) / 448.0).astype(np.float32)
    Wg_scale = (np.abs(Wg).reshape(D // B, B, F // B, B).max(axis=(1, 3)) / 448.0).astype(np.float32)
    X_bytes = e4m3fn_bytes(X / np.repeat(f64(X_scale), B, axis=1))
    Wg_bytes = e4m3fn_bytes(Wg / np.repeat(np.repeat(f64(Wg_scale), B, axis=0), B, axis=1))
    A = bf(np.random.standard_normal((H, T, E)) * t.reshape(H, 1, E))
    Wo_words, Wo_scales = pack4(np.random.standard_normal((F, D)) / np.sqrt(F) / t[:, None])
    return {"X_bytes": X_bytes, "X_scale": X_scale, "Wg_bytes": Wg_bytes, "Wg_scale": Wg_scale,
            "A": A, "Wo_words": Wo_words, "Wo_scales": Wo_scales}


def reference(X_bytes, X_scale, Wg_bytes, Wg_scale, A, Wo_words, Wo_scales):
    X = e4m3fn_values(X_bytes) * np.repeat(f64(X_scale), B, axis=1)
    Wg = e4m3fn_values(Wg_bytes) * np.repeat(np.repeat(f64(Wg_scale), B, axis=0), B, axis=1)
    z = mxq(X, 1, "e4m3") @ mxq(Wg, 0, "e4m3")
    gate = 1.0 / (1.0 + np.exp(-z))
    a = f64(A).transpose(1, 0, 2).reshape(T, F)
    h = a * gate
    y = mxq(h, 1, "e4m3") @ unpack4(Wo_words, Wo_scales)
    return y

@@ -1,0 +1,362 @@
+from contextlib import ExitStack
+
+import concourse.mybir as mybir
+from concourse.masks import make_identity
+
+F32 = mybir.dt.float32
+BF16 = mybir.dt.bfloat16
+U32 = mybir.dt.uint32
+I32 = mybir.dt.int32
+U8 = mybir.dt.uint8
+E4M3 = mybir.dt.float8_e4m3fn
+E4M3_X4 = mybir.dt.float8_e4m3fn_x4
+E2M1_X4 = mybir.dt.float4_e2m1fn_x4
+MULT = mybir.AluOpType.mult
+COPY = mybir.ActivationFunctionType.Copy
+SIGMOID = mybir.ActivationFunctionType.Sigmoid
+
+P = 128
+T, D, F = 512, 1536, 2048
+FLOPS = 2 * 2 * T * D * F
+SLOTS = 4
+PASS = P * SLOTS
+NS = T // P
+NG = D // PASS
+NF = F // PASS
+NN = D // 512
+NC = NF * NG
+SCALE_BLOCK = 128
+HEADS = 16
+
+SCALAR_BLOCKS = {1: 8}
+LEAD = 3
+
+TURN_A = {4: [(2, 0)], 7: [(2, 1)], 8: [(3, 0)], 11: [(3, 1)]}
+COPY_A = {2: [(0, 0), (0, 1)], 3: [(1, 0)], 6: [(1, 1), (2, 0)], 8: [(2, 1)], 10: [(3, 0)], NC: [(3, 1)]}
+GATES = {7: (0, 0), 8: (1, 0)}
+OUT_BANKS = ((5, 6, 7), (0, 1, 2), (3, 5, 6), (7, 0, 1))
+
+
+def tile_sigmoid_gated_attention_output_d4_kernel(
+    tc, X_bytes, X_scale, Wg_bytes, Wg_scale, A, Wo_words, Wo_scales, out
+):
+    nc = tc.nc
+    with ExitStack() as ctx:
+        keep = ctx.enter_context(tc.tile_pool(name="keep", bufs=1))
+        stage = ctx.enter_context(tc.tile_pool(name="stage", bufs=3))
+        psum = ctx.enter_context(tc.psum_pool(name="psum", bufs=1))
+
+        def bank(i, name):
+            return psum.tile([P, 512], F32, name=name, tag="bank%d" % i)
+
+        def keep_list(count, shape, dtype, name):
+            return [keep.tile(shape, dtype, name="%s%d" % (name, i), align_bytes=64) for i in range(count)]
+
+        x_bytes = keep_list(NS, [P, D], U8, "x_bytes")
+        x_values = keep_list(NS, [P, D], BF16, "x_values")
+        x_words = keep_list(NG, [P, SLOTS * T], BF16, "x_words")
+        x_codes = keep_list(NG, [P, T], U32, "x_codes")
+        x_code_scales = keep_list(NG, [P, T], U8, "x_code_scales")
+        x_scale = keep.tile([P, NS, D // SCALE_BLOCK], F32, name="x_scale", align_bytes=64)
+        w_codes = keep_list(NC, [P, PASS], U32, "w_codes")
+        w_code_scales = keep_list(NC, [P, PASS], U8, "w_code_scales")
+        wg_scale = keep.tile([P, NG, F // SCALE_BLOCK], F32, name="wg_scale", align_bytes=64)
+        a_rows = keep_list(NS, [P, F], BF16, "a_rows")
+        a_turned = keep_list(NS, [P, NF, SLOTS * P], BF16, "a_turned")
+        gate_values = keep_list(NF, [P, SLOTS, T], F32, "gate_values")
+        h_codes = keep_list(NF, [P, T], U32, "h_codes")
+        h_code_scales = keep_list(NF, [P, T], U8, "h_code_scales")
+        wo_codes = keep_list(NF, [P, 2 * D], U8, "wo_codes")
+        wo_code_scales = keep.tile([P, NF, D], U8, name="wo_code_scales", align_bytes=64)
+        ident = keep.tile([P, P], F32, name="ident")
+        warm = keep.tile([P, 2], F32, name="warm")
+
+        nc.gpsimd.memset(warm[:], 0.0)
+        make_identity(nc, ident[:])
+        nc.gpsimd.memset(wo_code_scales[:].rearrange("p g n -> p (g n)").bitcast(I32), 0)
+
+        w_bytes = {}
+
+        def load_x_scale():
+            nc.scalar.dma_start(out=x_scale[:], in_=X_scale.rearrange("(p s) j -> p s j", s=NS))
+
+        def load_x(s):
+            nc.sync.dma_start(out=x_bytes[s][:], in_=X_bytes.rearrange("(p s) k -> s p k", s=NS)[s])
+
+        def load_w(c):
+            G, g = divmod(c, NG)
+            w_bytes[c] = stage.tile([P, SLOTS * 512], U8, name="w_bytes", tag="w_bytes", bufs=8, align_bytes=64)
+            nc.sync.dma_start(
+                out=w_bytes[c][:].rearrange("p (j n) -> p j n", j=SLOTS),
+                in_=Wg_bytes[PASS * g : PASS * (g + 1), 512 * G : 512 * (G + 1)].rearrange("(p j) n -> p j n", j=SLOTS),
+            )
+
+        def load_wg_scale():
+            for q in range(4):
+                nc.sync.dma_start(
+                    out=wg_scale[32 * q : 32 * (q + 1), :, :],
+                    in_=Wg_scale.rearrange("(g q) b -> q g b", q=4)[q].partition_broadcast(32),
+                )
+
+        def load_a(s):
+            nc.sync.dma_start(
+                out=a_rows[s][:].rearrange("p (c e) -> p c e", c=HEADS),
+                in_=A.rearrange("c (p s) e -> s p c e", s=NS)[s],
+            )
+
+        def load_wo(G):
+            nc.sync.dma_start(out=wo_codes[G][:], in_=Wo_words[G])
+
+        def load_wo_scales():
+            for q in range(4):
+                nc.sync.dma_start(
+                    out=wo_code_scales[32 * q : 32 * q + 4, :, :].bitcast(I32),
+                    in_=Wo_scales.rearrange("g (q r) n -> q r g n", r=4)[q].bitcast(I32),
+                )
+
+        x_turned = {}
+
+        def scale_x(s):
+            for j in range(D // SCALE_BLOCK):
+                cols = slice(SCALE_BLOCK * j, SCALE_BLOCK * (j + 1))
+                values = x_values[s][:, cols]
+                codes = x_bytes[s][:, cols].bitcast(E4M3)
+                if j < SCALAR_BLOCKS.get(s, 0):
+                    nc.scalar.activation(out=values, in_=codes, func=COPY, scale=x_scale[:, s, j : j + 1])
+                else:
+                    nc.vector.tensor_scalar(
+                        out=values, in0=codes, scalar1=x_scale[:, s, j : j + 1], scalar2=None, op0=MULT
+                    )
+
+        def transpose_words(dst, rows, group):
+            words = rows.bitcast(F32)
+            for u in range(2):
+                nc.tensor.transpose(dst[u], words[:, 256 * group + u : 256 * (group + 1) : 2], ident[:])
+
+        def turn_x(half):
+            for g in range(NG):
+                x_turned[half, g] = bank(NG * half + g, "x_turned")
+                for i in range(2):
+                    dst = [x_turned[half, g][:, 256 * u + P * i : 256 * u + P * (i + 1)] for u in range(2)]
+                    transpose_words(dst, x_values[2 * half + i][:], g)
+
+        def copy_x(half):
+            for g in range(NG):
+                nc.scalar.copy(
+                    out=x_words[g][:, 1024 * half : 1024 * (half + 1)].bitcast(F32).rearrange("p (r u) -> p r u", u=2),
+                    in_=x_turned[half, g][:].rearrange("p (u r) -> p r u", u=2),
+                )
+
+        def quantize_x(half):
+            for g in range(NG):
+                cols = slice(256 * half, 256 * (half + 1))
+                nc.vector.quantize_mx(
+                    out=x_codes[g][:, cols].bitcast(E4M3_X4),
+                    scales=x_code_scales[g][:, cols],
+                    in_=x_words[g][:, 1024 * half : 1024 * (half + 1)],
+                )
+
+        w_wide, w_words = {}, {}
+
+        def widen(c):
+            w_wide[c] = stage.tile([P, SLOTS * 512], BF16, name="w_wide", tag="w_wide", bufs=6, align_bytes=64)
+            nc.scalar.copy(out=w_wide[c][:], in_=w_bytes[c][:].bitcast(E4M3))
+
+        def weave(c, blocks):
+            G, g = divmod(c, NG)
+            if c not in w_words:
+                w_words[c] = stage.tile([P, SLOTS * 512], BF16, name="w_words", tag="w_words", align_bytes=64)
+            dst = w_words[c][:].rearrange("p (t m j) -> p m j t", t=SLOTS, j=SLOTS)
+            src = w_wide[c][:].rearrange("p (j m t) -> p m j t", j=SLOTS, t=SLOTS)
+            for b in blocks:
+                rows = slice(32 * b, 32 * (b + 1))
+                nc.vector.tensor_scalar(
+                    out=dst[:, rows],
+                    in0=src[:, rows],
+                    scalar1=wg_scale[:, g, 4 * G + b : 4 * G + b + 1],
+                    scalar2=None,
+                    op0=MULT,
+                )
+
+        def quantize_w(c):
+            nc.vector.quantize_mx(out=w_codes[c][:].bitcast(E4M3_X4), scales=w_code_scales[c][:], in_=w_words[c][:])
+
+        z = {}
+
+        def multiply_z(c):
+            G, g = divmod(c, NG)
+            for t in range(SLOTS):
+                if g == 0:
+                    z[G, t] = bank(t, "z")
+                cols = slice(P * t, P * (t + 1))
+                nc.tensor.matmul_mx(
+                    out=z[G, t][:],
+                    lhsT=w_codes[c][:, cols].bitcast(E4M3_X4),
+                    lhsT_scale=w_code_scales[c][:, cols],
+                    rhs=x_codes[g][:].bitcast(E4M3_X4),
+                    rhs_scale=x_code_scales[g][:],
+                    start=(g == 0),
+                    stop=(g == NG - 1),
+                )
+
+        def sigmoid(G, tokens):
+            for t in range(SLOTS):
+                nc.scalar.activation(out=gate_values[G][:, t, tokens], in_=z[G, t][:, tokens], func=SIGMOID)
+
+        a_banks = {}
+
+        def turn_a(i, s, half):
+            a_banks[s, half] = bank(i, "a_bank")
+            for k in range(2):
+                dst = [a_banks[s, half][:, 256 * k + P * u : 256 * k + P * (u + 1)] for u in range(2)]
+                transpose_words(dst, a_rows[s][:], 2 * half + k)
+
+        def copy_a(s, half):
+            nc.scalar.copy(
+                out=a_turned[s][:, 2 * half : 2 * half + 2, :].bitcast(F32).rearrange("p k (r u) -> p k r u", u=2),
+                in_=a_banks[s, half][:].rearrange("p (k u r) -> p k r u", k=2, u=2),
+            )
+
+        h_words, y = {}, {}
+
+        def gate(G, s):
+            h_words[G, s] = stage.tile([P, SLOTS * P], BF16, name="h_words", tag="h_words", align_bytes=64)
+            nc.vector.tensor_tensor(
+                out=h_words[G, s][:].rearrange("p (c i t) -> p c t i", i=4, t=SLOTS),
+                in0=gate_values[G][:, :, P * s : P * (s + 1)].rearrange("p t (c i) -> p c t i", i=4),
+                in1=a_turned[s][:, G, :].rearrange("p (c i t) -> p c t i", i=4, t=SLOTS),
+                op=MULT,
+            )
+
+        def quantize_h(G, s):
+            cols = slice(P * s, P * (s + 1))
+            nc.vector.quantize_mx(
+                out=h_codes[G][:, cols].bitcast(E4M3_X4), scales=h_code_scales[G][:, cols], in_=h_words[G, s][:]
+            )
+
+        def multiply_y(G, s, n):
+            if G == 0:
+                y[s, n] = bank(OUT_BANKS[s][n], "y")
+            cols = slice(P * s, P * (s + 1))
+            nc.tensor.matmul_mx(
+                out=y[s, n][:],
+                lhsT=h_codes[G][:, cols].bitcast(E4M3_X4),
+                lhsT_scale=h_code_scales[G][:, cols],
+                rhs=wo_codes[G][:, 1024 * n : 1024 * (n + 1)].bitcast(E2M1_X4),
+                rhs_scale=wo_code_scales[:, G, 512 * n : 512 * (n + 1)],
+                start=(G == 0),
+                stop=(G == NF - 1),
+            )
+
+        def store_y(s, n, pieces):
+            width = 512 // pieces
+            for lo in range(0, 512, width):
+                y_rows = stage.tile([P, 512], F32, name="y_rows", tag="y_rows", bufs=6, align_bytes=64)
+                nc.scalar.copy(out=y_rows[:, :width], in_=y[s, n][:, lo : lo + width])
+                nc.sync.dma_start(
+                    out=out.rearrange("(p s) n -> s p n", s=NS)[s][:, 512 * n + lo : 512 * n + lo + width],
+                    in_=y_rows[:, :width],
+                )
+
+        def add_to_y(G, s):
+            last_tile = s == NS - 1
+            for n in range(NN - 1 if last_tile else NN):
+                multiply_y(G, s, n)
+                if G == NF - 1:
+                    store_y(s, n, 1)
+            if last_tile and G == NF - 1:
+                for k in range(NF):
+                    multiply_y(k, s, NN - 1)
+                store_y(s, NN - 1, 2)
+
+        with tc.manual_schedule():
+            load_x_scale()
+            nc.scalar.activation(out=warm[:, 1:2], in_=warm[:, 0:1], func=SIGMOID)
+            load_x(1)
+            load_x(0)
+            load_w(0)
+            load_x(3)
+            load_w(1)
+            load_x(2)
+            load_w(2)
+            load_wg_scale()
+            load_a(0)
+            load_w(3)
+            load_w(4)
+            load_a(1)
+            load_w(5)
+            load_w(6)
+            load_w(7)
+            load_a(2)
+            load_w(8)
+            load_w(9)
+            load_wo_scales()
+            load_wo(0)
+            load_w(10)
+            load_a(3)
+            load_wo(1)
+            load_w(11)
+            load_wo(2)
+            load_wo(3)
+
+            scale_x(1)
+            scale_x(0)
+            turn_x(0)
+            widen(0)
+            widen(1)
+            scale_x(3)
+            copy_x(0)
+            scale_x(2)
+            turn_x(1)
+            copy_x(1)
+            weave(0, range(4))
+            weave(1, range(4))
+            turn_a(7, 0, 1)
+            turn_a(6, 0, 0)
+            quantize_x(0)
+            quantize_w(0)
+            quantize_x(1)
+            quantize_w(1)
+            for c in range(2, 2 + LEAD):
+                widen(c)
+            multiply_z(0)
+            turn_a(5, 1, 1)
+            turn_a(4, 1, 0)
+            weave(2, range(4))
+            multiply_z(1)
+
+            for c in range(2, NC):
+                G, g = divmod(c, NG)
+                if g == 0:
+                    sigmoid(G - 1, slice(0, T))
+                if c + LEAD < NC:
+                    widen(c + LEAD)
+                for s, half in COPY_A.get(c, []):
+                    copy_a(s, half)
+                if c + 1 < NC:
+                    weave(c + 1, (0, 1))
+                if c in GATES:
+                    gate(*GATES[c])
+                quantize_w(c)
+                multiply_z(c)
+                for s, half in TURN_A.get(c, []):
+                    turn_a(4, s, half)
+                if c + 1 < NC:
+                    weave(c + 1, (2, 3))
+                if c in GATES:
+                    quantize_h(*GATES[c])
+                    add_to_y(*GATES[c])
+
+            for lo in (0, T // 2):
+                sigmoid(NF - 1, slice(lo, lo + T // 2))
+            for s, half in COPY_A[NC]:
+                copy_a(s, half)
+            rest = [(G, s) for s in (0, 1) for G in range(NF - 1)] + [(NF - 1, 0), (NF - 1, 1)]
+            rest += [(G, s) for s in (2, 3) for G in range(NF)]
+            rest = [k for k in rest if k not in GATES.values()]
+            gate(*rest[0])
+            for i, done in enumerate(rest):
+                if i + 1 < len(rest):
+                    gate(*rest[i + 1])
+                quantize_h(*done)
+                add_to_y(*done)

@@ -63,7 +63,7 @@ def tile_sigmoid_gated_attention_output_d4_kernel(
         wg_scale = keep.tile([P, NG, F // SCALE_BLOCK], F32, name="wg_scale", align_bytes=64)
         a_rows = keep_list(NS, [P, F], BF16, "a_rows")
         a_turned = keep_list(NS, [P, NF, SLOTS * P], BF16, "a_turned")
-        gate_values = keep_list(NF, [P, SLOTS, T], F32, "gate_values")
+        gate_values = keep_list(NF, [P, 2, T, 2], F32, "gate_values")
         h_codes = keep_list(NF, [P, T], U32, "h_codes")
         h_code_scales = keep_list(NF, [P, T], U8, "h_code_scales")
         wo_codes = keep_list(NF, [P, 2 * D], U8, "wo_codes")
@@ -185,23 +185,31 @@ def tile_sigmoid_gated_attention_output_d4_kernel(
 
         def multiply_z(c):
             G, g = divmod(c, NG)
-            for t in range(SLOTS):
-                if g == 0:
-                    z[G, t] = bank(t, "z")
-                cols = slice(P * t, P * (t + 1))
-                nc.tensor.matmul_mx(
-                    out=z[G, t][:],
-                    lhsT=w_codes[c][:, cols].bitcast(E4M3_X4),
-                    lhsT_scale=w_code_scales[c][:, cols],
-                    rhs=x_codes[g][:].bitcast(E4M3_X4),
-                    rhs_scale=x_code_scales[g][:],
-                    start=(g == 0),
-                    stop=(g == NG - 1),
-                )
+            for half in range(2):
+                tokens = slice(256 * half, 256 * (half + 1))
+                for t in range(SLOTS):
+                    pair, e = divmod(t, 2)
+                    if g == 0 and e == 0:
+                        z[G, half, pair] = bank(2 * half + pair, "z")
+                    cols = slice(P * t, P * (t + 1))
+                    nc.tensor.matmul_mx(
+                        out=z[G, half, pair][:, 256 * e : 256 * (e + 1)],
+                        lhsT=w_codes[c][:, cols].bitcast(E4M3_X4),
+                        lhsT_scale=w_code_scales[c][:, cols],
+                        rhs=x_codes[g][:, tokens].bitcast(E4M3_X4),
+                        rhs_scale=x_code_scales[g][:, tokens],
+                        start=(g == 0 and e == 0),
+                        stop=(g == NG - 1 and e == 1),
+                    )
 
-        def sigmoid(G, tokens):
-            for t in range(SLOTS):
-                nc.scalar.activation(out=gate_values[G][:, t, tokens], in_=z[G, t][:, tokens], func=SIGMOID)
+        def sigmoid(G, lo, count):
+            half, first = divmod(lo, 256)
+            for pair in range(2):
+                nc.scalar.activation(
+                    out=gate_values[G][:, pair, lo : lo + count, :],
+                    in_=z[G, half, pair][:].rearrange("p (e r) -> p r e", e=2)[:, first : first + count, :],
+                    func=SIGMOID,
+                )
 
         a_banks = {}
 
@@ -222,9 +230,9 @@ def tile_sigmoid_gated_attention_output_d4_kernel(
         def gate(G, s):
             h_words[G, s] = stage.tile([P, SLOTS * P], BF16, name="h_words", tag="h_words", align_bytes=64)
             nc.vector.tensor_tensor(
-                out=h_words[G, s][:].rearrange("p (c i t) -> p c t i", i=4, t=SLOTS),
-                in0=gate_values[G][:, :, P * s : P * (s + 1)].rearrange("p t (c i) -> p c t i", i=4),
-                in1=a_turned[s][:, G, :].rearrange("p (c i t) -> p c t i", i=4, t=SLOTS),
+                out=h_words[G, s][:].rearrange("p (r k e) -> p r k e", k=2, e=2),
+                in0=gate_values[G][:, :, P * s : P * (s + 1), :].rearrange("p k r e -> p r k e"),
+                in1=a_turned[s][:, G, :].rearrange("p (r k e) -> p r k e", k=2, e=2),
                 op=MULT,
             )
 
@@ -328,7 +336,8 @@ def tile_sigmoid_gated_attention_output_d4_kernel(
             for c in range(2, NC):
                 G, g = divmod(c, NG)
                 if g == 0:
-                    sigmoid(G - 1, slice(0, T))
+                    for lo in (0, T // 2):
+                        sigmoid(G - 1, lo, T // 2)
                 if c + LEAD < NC:
                     widen(c + LEAD)
                 for s, half in COPY_A.get(c, []):
@@ -348,7 +357,7 @@ def tile_sigmoid_gated_attention_output_d4_kernel(
                     add_to_y(*GATES[c])
 
             for lo in (0, T // 2):
-                sigmoid(NF - 1, slice(lo, lo + T // 2))
+                sigmoid(NF - 1, lo, T // 2)
             for s, half in COPY_A[NC]:
                 copy_a(s, half)
             rest = [(G, s) for s in (0, 1) for G in range(NF - 1)] + [(NF - 1, 0), (NF - 1, 1)]

@@ -28,13 +28,16 @@ NC = NF * NG
 SCALE_BLOCK = 128
 HEADS = 16
 
-SCALAR_BLOCKS = {1: 8}
-LEAD = 3
-
-TURN_A = {4: [(2, 0)], 7: [(2, 1)], 8: [(3, 0)], 11: [(3, 1)]}
-COPY_A = {2: [(0, 0), (0, 1)], 3: [(1, 0)], 6: [(1, 1), (2, 0)], 8: [(2, 1)], 10: [(3, 0)], NC: [(3, 1)]}
-GATES = {7: (0, 0), 8: (1, 0)}
-OUT_BANKS = ((5, 6, 7), (0, 1, 2), (3, 5, 6), (7, 0, 1))
+SCALAR_TILES = (0, 1)
+LEAD = 4
+A_AFTER = (3, 5, 7, 9)
+A_BANKS = (6, 4, 4, 6)
+TURN_A = {2: [1], 4: [2], 5: [3]}
+WIDEN = {1: 5, 2: 6, 3: 7, 4: 8, 5: 9, 6: 10, 8: 11}
+COPY_A = {2: [(0, 0), (0, 1)], 4: [(1, 0), (1, 1)], 8: [(2, 0), (2, 1)], 9: [(3, 0)], 10: [(3, 1)]}
+GATES = {4: 0, 7: 1, 9: 2}
+ADD_Y = {9: [0, 1], 10: [2]}
+OUT_BANKS = ((4, 5, 6), (7, 0, 1), (2, 3, 4), (5, 6, 7))
 
 
 def tile_sigmoid_gated_attention_output_d4_kernel(
@@ -116,16 +119,30 @@ def tile_sigmoid_gated_attention_output_d4_kernel(
 
         x_turned = {}
 
-        def scale_x(s):
+        def on_scalar(s, g):
+            return s in SCALAR_TILES and g == NG - 1
+
+        def scale_x(s, engine):
             for j in range(D // SCALE_BLOCK):
-                cols = slice(SCALE_BLOCK * j, SCALE_BLOCK * (j + 1))
-                values = x_values[s][:, cols]
-                codes = x_bytes[s][:, cols].bitcast(E4M3)
-                if j < SCALAR_BLOCKS.get(s, 0):
-                    nc.scalar.activation(out=values, in_=codes, func=COPY, scale=x_scale[:, s, j : j + 1])
+                g, q = divmod(j, SLOTS)
+                if on_scalar(s, g) != (engine is nc.scalar):
+                    continue
+                codes = x_bytes[s][:, SCALE_BLOCK * j : SCALE_BLOCK * (j + 1)].bitcast(E4M3)
+                values = x_values[s][:, PASS * g : PASS * (g + 1)]
+                if engine is nc.scalar:
+                    nc.scalar.activation(
+                        out=values[:, SCALE_BLOCK * q : SCALE_BLOCK * (q + 1)],
+                        in_=codes,
+                        func=COPY,
+                        scale=x_scale[:, s, j : j + 1],
+                    )
                 else:
                     nc.vector.tensor_scalar(
-                        out=values, in0=codes, scalar1=x_scale[:, s, j : j + 1], scalar2=None, op0=MULT
+                        out=values.rearrange("p (u m e) -> p m u e", u=2, e=2)[:, 32 * q : 32 * (q + 1)],
+                        in0=codes.rearrange("p (m u e) -> p m u e", u=2, e=2),
+                        scalar1=x_scale[:, s, j : j + 1],
+                        scalar2=None,
+                        op0=MULT,
                     )
 
         def transpose_words(dst, rows, group):
@@ -133,12 +150,18 @@ def tile_sigmoid_gated_attention_output_d4_kernel(
             for u in range(2):
                 nc.tensor.transpose(dst[u], words[:, 256 * group + u : 256 * (group + 1) : 2], ident[:])
 
-        def turn_x(half):
+        def turn_x(s):
+            half, i = divmod(s, 2)
             for g in range(NG):
-                x_turned[half, g] = bank(NG * half + g, "x_turned")
-                for i in range(2):
-                    dst = [x_turned[half, g][:, 256 * u + P * i : 256 * u + P * (i + 1)] for u in range(2)]
-                    transpose_words(dst, x_values[2 * half + i][:], g)
+                if i == 0:
+                    x_turned[half, g] = bank(NG * half + g, "x_turned")
+                dst = [x_turned[half, g][:, 256 * u + P * i : 256 * u + P * (i + 1)] for u in range(2)]
+                if on_scalar(s, g):
+                    transpose_words(dst, x_values[s][:], g)
+                else:
+                    words = x_values[s][:].bitcast(F32)
+                    for u in range(2):
+                        nc.tensor.transpose(dst[u], words[:, 256 * g + P * u : 256 * g + P * (u + 1)], ident[:])
 
         def copy_x(half):
             for g in range(NG):
@@ -183,9 +206,9 @@ def tile_sigmoid_gated_attention_output_d4_kernel(
 
         z = {}
 
-        def multiply_z(c):
+        def multiply_z(c, halves):
             G, g = divmod(c, NG)
-            for half in range(2):
+            for half in halves:
                 tokens = slice(256 * half, 256 * (half + 1))
                 for t in range(SLOTS):
                     pair, e = divmod(t, 2)
@@ -213,11 +236,12 @@ def tile_sigmoid_gated_attention_output_d4_kernel(
 
         a_banks = {}
 
-        def turn_a(i, s, half):
-            a_banks[s, half] = bank(i, "a_bank")
-            for k in range(2):
-                dst = [a_banks[s, half][:, 256 * k + P * u : 256 * k + P * (u + 1)] for u in range(2)]
-                transpose_words(dst, a_rows[s][:], 2 * half + k)
+        def turn_a(s):
+            for half in range(2):
+                a_banks[s, half] = bank(A_BANKS[s] + half, "a_bank")
+                for k in range(2):
+                    dst = [a_banks[s, half][:, 256 * k + P * u : 256 * k + P * (u + 1)] for u in range(2)]
+                    transpose_words(dst, a_rows[s][:], 2 * half + k)
 
         def copy_a(s, half):
             nc.scalar.copy(
@@ -280,89 +304,73 @@ def tile_sigmoid_gated_attention_output_d4_kernel(
         with tc.manual_schedule():
             load_x_scale()
             nc.scalar.activation(out=warm[:, 1:2], in_=warm[:, 0:1], func=SIGMOID)
-            load_x(1)
             load_x(0)
+            load_x(1)
             load_w(0)
-            load_x(3)
-            load_w(1)
             load_x(2)
-            load_w(2)
+            load_w(1)
+            load_x(3)
             load_wg_scale()
-            load_a(0)
-            load_w(3)
-            load_w(4)
-            load_a(1)
-            load_w(5)
-            load_w(6)
-            load_w(7)
-            load_a(2)
-            load_w(8)
-            load_w(9)
-            load_wo_scales()
-            load_wo(0)
-            load_w(10)
-            load_a(3)
-            load_wo(1)
-            load_w(11)
-            load_wo(2)
-            load_wo(3)
-
-            scale_x(1)
-            scale_x(0)
-            turn_x(0)
-            widen(0)
-            widen(1)
-            scale_x(3)
-            copy_x(0)
-            scale_x(2)
-            turn_x(1)
-            copy_x(1)
-            weave(0, range(4))
-            weave(1, range(4))
-            turn_a(7, 0, 1)
-            turn_a(6, 0, 0)
-            quantize_x(0)
-            quantize_w(0)
-            quantize_x(1)
-            quantize_w(1)
-            for c in range(2, 2 + LEAD):
-                widen(c)
-            multiply_z(0)
-            turn_a(5, 1, 1)
-            turn_a(4, 1, 0)
-            weave(2, range(4))
-            multiply_z(1)
-
             for c in range(2, NC):
+                load_w(c)
+                if c in A_AFTER:
+                    load_a(A_AFTER.index(c))
+            load_wo_scales()
+            for G in range(NF):
+                load_wo(G)
+
+            for s in range(NS):
+                scale_x(s, nc.scalar)
+                scale_x(s, nc.vector)
+                turn_x(s)
+                if s in (1, 2):
+                    widen(s - 1)
+            copy_x(0)
+            widen(2)
+            copy_x(1)
+            turn_a(0)
+            weave(0, range(4))
+            weave(1, (0, 1))
+            quantize_w(0)
+            weave(1, (2, 3))
+            quantize_x(0)
+            multiply_z(0, (0,))
+            for c in range(NG, 1 + LEAD):
+                widen(c)
+
+            for c in range(1, NC):
                 G, g = divmod(c, NG)
+                for s, half in COPY_A.get(c, []):
+                    copy_a(s, half)
                 if g == 0:
                     for lo in (0, T // 2):
                         sigmoid(G - 1, lo, T // 2)
-                if c + LEAD < NC:
-                    widen(c + LEAD)
-                for s, half in COPY_A.get(c, []):
-                    copy_a(s, half)
+                if c in WIDEN:
+                    widen(WIDEN[c])
                 if c + 1 < NC:
                     weave(c + 1, (0, 1))
-                if c in GATES:
-                    gate(*GATES[c])
+                if c - 1 in GATES:
+                    quantize_h(GATES[c - 1], 0)
                 quantize_w(c)
-                multiply_z(c)
-                for s, half in TURN_A.get(c, []):
-                    turn_a(4, s, half)
+                for G_done in ADD_Y.get(c, []):
+                    add_to_y(G_done, 0)
+                if c == 1:
+                    multiply_z(1, (0,))
+                    quantize_x(1)
+                    multiply_z(0, (1,))
+                    multiply_z(1, (1,))
+                else:
+                    multiply_z(c, (0, 1))
+                for s in TURN_A.get(c, []):
+                    turn_a(s)
                 if c + 1 < NC:
                     weave(c + 1, (2, 3))
                 if c in GATES:
-                    quantize_h(*GATES[c])
-                    add_to_y(*GATES[c])
+                    gate(GATES[c], 0)
 
-            for lo in (0, T // 2):
-                sigmoid(NF - 1, lo, T // 2)
-            for s, half in COPY_A[NC]:
-                copy_a(s, half)
-            rest = [(G, s) for s in (0, 1) for G in range(NF - 1)] + [(NF - 1, 0), (NF - 1, 1)]
-            rest += [(G, s) for s in (2, 3) for G in range(NF)]
-            rest = [k for k in rest if k not in GATES.values()]
+            for s in range(NS):
+                sigmoid(NF - 1, P * s, P)
+            rest = [(0, 1), (1, 1), (2, 1), (3, 0), (3, 1)] + [(G, s) for s in (2, 3) for G in range(NF)]
             gate(*rest[0])
             for i, done in enumerate(rest):
                 if i + 1 < len(rest):

@@ -27,17 +27,26 @@ NN = D // 512
 NC = NF * NG
 SCALE_BLOCK = 128
 HEADS = 16
+HALF = T // 2
 
-SCALAR_TILES = (0, 1)
+SCALAR_TILES = (0, 1, 3)
 LEAD = 4
-A_AFTER = (3, 5, 7, 9)
-A_BANKS = (6, 4, 4, 6)
-TURN_A = {2: [1], 4: [2], 5: [3]}
-WIDEN = {1: 5, 2: 6, 3: 7, 4: 8, 5: 9, 6: 10, 8: 11}
-COPY_A = {2: [(0, 0), (0, 1)], 4: [(1, 0), (1, 1)], 8: [(2, 0), (2, 1)], 9: [(3, 0)], 10: [(3, 1)]}
-GATES = {4: 0, 7: 1, 9: 2}
-ADD_Y = {9: [0, 1], 10: [2]}
-OUT_BANKS = ((4, 5, 6), (7, 0, 1), (2, 3, 4), (5, 6, 7))
+Z_BANKS = 4
+WO_AFTER = 9
+A_AFTER = {2: 2, 4: 3, 6: 0, 7: 1}
+A_BANKS = ((6, 7), (5, 4), (6, 7), (4, 5))
+A_IN_PSUM = ((0, 0), (1, 0))
+TURN_A = {2: [(3, 0), (3, 1)], 3: [(0, 0), (0, 1)], 4: [(1, 1), (1, 0)]}
+COPY_A = {2: [(2, 0), (2, 1)], 4: [(3, 0), (3, 1)], 5: [(0, 1), (1, 1)]}
+WIDEN = {1: [5], 2: [6], 3: [7], 4: [8], 5: [9], 6: [10], 7: [11]}
+SCALAR_WEAVES = {10: 2, 11: 1}
+SW0 = {8: [10]}
+SW = {9: [11]}
+GATES = {4: 0, 7: 1}
+ADD_Y = {7: [(0, 1), (0, 2)], 8: [(0, 0), (1, 0), (1, 1), (1, 2)]}
+TAILA = 256
+TAIL_BANK = 0
+OUT_BANKS = ((6, 7, 4), (5, 0, 1), (2, 3, 6), (7, 4, 5))
 
 
 def tile_sigmoid_gated_attention_output_d4_kernel(
@@ -65,10 +74,10 @@ def tile_sigmoid_gated_attention_output_d4_kernel(
         w_code_scales = keep_list(NC, [P, PASS], U8, "w_code_scales")
         wg_scale = keep.tile([P, NG, F // SCALE_BLOCK], F32, name="wg_scale", align_bytes=64)
         a_rows = keep_list(NS, [P, F], BF16, "a_rows")
-        a_turned = keep_list(NS, [P, NF, SLOTS * P], BF16, "a_turned")
-        gate_values = keep_list(NF, [P, 2, T, 2], F32, "gate_values")
-        h_codes = keep_list(NF, [P, T], U32, "h_codes")
-        h_code_scales = keep_list(NF, [P, T], U8, "h_code_scales")
+        a_turned = keep_list(NS, [P, NF * SLOTS * P], BF16, "a_turned")
+        gate_values = keep.tile([P, NS, 2, NF * P, 2], F32, name="gate_values", align_bytes=64)
+        h_codes = keep_list(NS, [P, NF * P], U32, "h_codes")
+        h_code_scales = keep_list(NS, [P, NF * P], U8, "h_code_scales")
         wo_codes = keep_list(NF, [P, 2 * D], U8, "wo_codes")
         wo_code_scales = keep.tile([P, NF, D], U8, name="wo_code_scales", align_bytes=64)
         ident = keep.tile([P, P], F32, name="ident")
@@ -111,10 +120,10 @@ def tile_sigmoid_gated_attention_output_d4_kernel(
             nc.sync.dma_start(out=wo_codes[G][:], in_=Wo_words[G])
 
         def load_wo_scales():
-            for q in range(4):
+            for r in range(4):
                 nc.sync.dma_start(
-                    out=wo_code_scales[32 * q : 32 * q + 4, :, :].bitcast(I32),
-                    in_=Wo_scales.rearrange("g (q r) n -> q r g n", r=4)[q].bitcast(I32),
+                    out=wo_code_scales[r:P:32, :, :].bitcast(I32),
+                    in_=Wo_scales.rearrange("g (q r) n -> r q g n", r=4)[r].bitcast(I32),
                 )
 
         x_turned = {}
@@ -185,38 +194,44 @@ def tile_sigmoid_gated_attention_output_d4_kernel(
             w_wide[c] = stage.tile([P, SLOTS * 512], BF16, name="w_wide", tag="w_wide", bufs=6, align_bytes=64)
             nc.scalar.copy(out=w_wide[c][:], in_=w_bytes[c][:].bitcast(E4M3))
 
-        def weave(c, blocks):
+        def weave(c, blocks, engine):
             G, g = divmod(c, NG)
             if c not in w_words:
-                w_words[c] = stage.tile([P, SLOTS * 512], BF16, name="w_words", tag="w_words", align_bytes=64)
+                w_words[c] = stage.tile([P, SLOTS * 512], BF16, name="w_words", tag="w_words", bufs=4, align_bytes=64)
             dst = w_words[c][:].rearrange("p (t m j) -> p m j t", t=SLOTS, j=SLOTS)
             src = w_wide[c][:].rearrange("p (j m t) -> p m j t", j=SLOTS, t=SLOTS)
             for b in blocks:
+                if (b >= SLOTS - SCALAR_WEAVES.get(c, 0)) != (engine is nc.scalar):
+                    continue
                 rows = slice(32 * b, 32 * (b + 1))
-                nc.vector.tensor_scalar(
-                    out=dst[:, rows],
-                    in0=src[:, rows],
-                    scalar1=wg_scale[:, g, 4 * G + b : 4 * G + b + 1],
-                    scalar2=None,
-                    op0=MULT,
-                )
+                scale = wg_scale[:, g, 4 * G + b : 4 * G + b + 1]
+                if engine is nc.scalar:
+                    nc.scalar.activation(out=dst[:, rows], in_=src[:, rows], func=COPY, scale=scale)
+                else:
+                    nc.vector.tensor_scalar(out=dst[:, rows], in0=src[:, rows], scalar1=scale, scalar2=None, op0=MULT)
 
-        def quantize_w(c):
-            nc.vector.quantize_mx(out=w_codes[c][:].bitcast(E4M3_X4), scales=w_code_scales[c][:], in_=w_words[c][:])
+        def quantize_w(c, pieces=1):
+            width = PASS // pieces
+            for lo in range(0, PASS, width):
+                nc.vector.quantize_mx(
+                    out=w_codes[c][:, lo : lo + width].bitcast(E4M3_X4),
+                    scales=w_code_scales[c][:, lo : lo + width],
+                    in_=w_words[c][:, SLOTS * lo : SLOTS * (lo + width)],
+                )
 
         z = {}
 
-        def multiply_z(c, halves):
+        def multiply_z(c, banks):
             G, g = divmod(c, NG)
-            for half in halves:
-                tokens = slice(256 * half, 256 * (half + 1))
-                for t in range(SLOTS):
-                    pair, e = divmod(t, 2)
-                    if g == 0 and e == 0:
-                        z[G, half, pair] = bank(2 * half + pair, "z")
-                    cols = slice(P * t, P * (t + 1))
+            for i in banks:
+                half, pair = divmod(i, 2)
+                tokens = slice(HALF * half, HALF * (half + 1))
+                if g == 0:
+                    z[G, half, pair] = bank(i, "z")
+                for e in range(2):
+                    cols = slice(P * (2 * pair + e), P * (2 * pair + e + 1))
                     nc.tensor.matmul_mx(
-                        out=z[G, half, pair][:, 256 * e : 256 * (e + 1)],
+                        out=z[G, half, pair][:, HALF * e : HALF * (e + 1)],
                         lhsT=w_codes[c][:, cols].bitcast(E4M3_X4),
                         lhsT_scale=w_code_scales[c][:, cols],
                         rhs=x_codes[g][:, tokens].bitcast(E4M3_X4),
@@ -225,81 +240,75 @@ def tile_sigmoid_gated_attention_output_d4_kernel(
                         stop=(g == NG - 1 and e == 1),
                     )
 
-        def sigmoid(G, lo, count):
-            half, first = divmod(lo, 256)
-            for pair in range(2):
-                nc.scalar.activation(
-                    out=gate_values[G][:, pair, lo : lo + count, :],
-                    in_=z[G, half, pair][:].rearrange("p (e r) -> p r e", e=2)[:, first : first + count, :],
-                    func=SIGMOID,
-                )
+        def sigmoid(G):
+            for half in range(2):
+                for pair in range(2):
+                    nc.scalar.activation(
+                        out=gate_values[:, 2 * half : 2 * half + 2, pair, P * G : P * (G + 1), :],
+                        in_=z[G, half, pair][:].rearrange("p (e i r) -> p i r e", e=2, i=2),
+                        func=SIGMOID,
+                    )
 
         a_banks = {}
 
-        def turn_a(s):
-            for half in range(2):
-                a_banks[s, half] = bank(A_BANKS[s] + half, "a_bank")
-                for k in range(2):
-                    dst = [a_banks[s, half][:, 256 * k + P * u : 256 * k + P * (u + 1)] for u in range(2)]
-                    transpose_words(dst, a_rows[s][:], 2 * half + k)
+        def turn_a(s, half):
+            a_banks[s, half] = bank(A_BANKS[s][half], "a_bank")
+            for k in range(2):
+                dst = [a_banks[s, half][:, 256 * u + P * k : 256 * u + P * (k + 1)] for u in range(2)]
+                transpose_words(dst, a_rows[s][:], 2 * half + k)
 
         def copy_a(s, half):
             nc.scalar.copy(
-                out=a_turned[s][:, 2 * half : 2 * half + 2, :].bitcast(F32).rearrange("p k (r u) -> p k r u", u=2),
-                in_=a_banks[s, half][:].rearrange("p (k u r) -> p k r u", k=2, u=2),
+                out=a_turned[s][:, 1024 * half : 1024 * (half + 1)].bitcast(F32).rearrange("p (r u) -> p r u", u=2),
+                in_=a_banks[s, half][:].rearrange("p (u r) -> p r u", u=2),
             )
 
         h_words, y = {}, {}
 
-        def gate(G, s):
-            h_words[G, s] = stage.tile([P, SLOTS * P], BF16, name="h_words", tag="h_words", align_bytes=64)
+        def gate(s, G, groups):
+            half, k = divmod(G, 2)
+            if (s, half) in A_IN_PSUM:
+                a_values = a_banks[s, half][:].bitcast(BF16).rearrange("p (u r e) -> p r u e", u=2, e=2)
+            else:
+                a_values = a_turned[s][:, 1024 * half : 1024 * (half + 1)].rearrange("p (r u e) -> p r u e", u=2, e=2)
+            h_words[s, G] = stage.tile([P, SLOTS * P * groups], BF16, name="h_words", tag="h_words", align_bytes=64)
             nc.vector.tensor_tensor(
-                out=h_words[G, s][:].rearrange("p (r k e) -> p r k e", k=2, e=2),
-                in0=gate_values[G][:, :, P * s : P * (s + 1), :].rearrange("p k r e -> p r k e"),
-                in1=a_turned[s][:, G, :].rearrange("p (r k e) -> p r k e", k=2, e=2),
+                out=h_words[s, G][:].rearrange("p (r u e) -> p r u e", u=2, e=2),
+                in0=gate_values[:, s, :, P * G : P * (G + groups), :].rearrange("p u r e -> p r u e"),
+                in1=a_values[:, P * k : P * (k + groups)],
                 op=MULT,
             )
 
-        def quantize_h(G, s):
-            cols = slice(P * s, P * (s + 1))
+        def quantize_h(s, G, groups):
+            cols = slice(P * G, P * (G + groups))
             nc.vector.quantize_mx(
-                out=h_codes[G][:, cols].bitcast(E4M3_X4), scales=h_code_scales[G][:, cols], in_=h_words[G, s][:]
+                out=h_codes[s][:, cols].bitcast(E4M3_X4), scales=h_code_scales[s][:, cols], in_=h_words[s, G][:]
             )
 
         def multiply_y(G, s, n):
             if G == 0:
                 y[s, n] = bank(OUT_BANKS[s][n], "y")
-            cols = slice(P * s, P * (s + 1))
+            add_pass(y[s, n][:], G, s, 512 * n, 512)
+
+        def add_pass(dst, G, s, lo, width):
+            cols = slice(P * G, P * (G + 1))
             nc.tensor.matmul_mx(
-                out=y[s, n][:],
-                lhsT=h_codes[G][:, cols].bitcast(E4M3_X4),
-                lhsT_scale=h_code_scales[G][:, cols],
-                rhs=wo_codes[G][:, 1024 * n : 1024 * (n + 1)].bitcast(E2M1_X4),
-                rhs_scale=wo_code_scales[:, G, 512 * n : 512 * (n + 1)],
+                out=dst,
+                lhsT=h_codes[s][:, cols].bitcast(E4M3_X4),
+                lhsT_scale=h_code_scales[s][:, cols],
+                rhs=wo_codes[G][:, 2 * lo : 2 * (lo + width)].bitcast(E2M1_X4),
+                rhs_scale=wo_code_scales[:, G, lo : lo + width],
                 start=(G == 0),
                 stop=(G == NF - 1),
             )
 
-        def store_y(s, n, pieces):
-            width = 512 // pieces
-            for lo in range(0, 512, width):
-                y_rows = stage.tile([P, 512], F32, name="y_rows", tag="y_rows", bufs=6, align_bytes=64)
-                nc.scalar.copy(out=y_rows[:, :width], in_=y[s, n][:, lo : lo + width])
-                nc.sync.dma_start(
-                    out=out.rearrange("(p s) n -> s p n", s=NS)[s][:, 512 * n + lo : 512 * n + lo + width],
-                    in_=y_rows[:, :width],
-                )
-
-        def add_to_y(G, s):
-            last_tile = s == NS - 1
-            for n in range(NN - 1 if last_tile else NN):
-                multiply_y(G, s, n)
-                if G == NF - 1:
-                    store_y(s, n, 1)
-            if last_tile and G == NF - 1:
-                for k in range(NF):
-                    multiply_y(k, s, NN - 1)
-                store_y(s, NN - 1, 2)
+        def store_y(src, s, lo, width, engine):
+            y_rows = stage.tile([P, width], F32, name="y_rows", tag="w_wide", bufs=6, align_bytes=64)
+            if engine is nc.scalar:
+                nc.scalar.copy(out=y_rows[:], in_=src)
+            else:
+                nc.vector.tensor_copy(out=y_rows[:], in_=src)
+            nc.sync.dma_start(out=out.rearrange("(p s) n -> s p n", s=NS)[s][:, lo : lo + width], in_=y_rows[:])
 
         with tc.manual_schedule():
             load_x_scale()
@@ -308,72 +317,104 @@ def tile_sigmoid_gated_attention_output_d4_kernel(
             load_x(1)
             load_w(0)
             load_x(2)
-            load_w(1)
             load_x(3)
+            load_w(1)
             load_wg_scale()
             for c in range(2, NC):
                 load_w(c)
                 if c in A_AFTER:
-                    load_a(A_AFTER.index(c))
-            load_wo_scales()
-            for G in range(NF):
-                load_wo(G)
+                    load_a(A_AFTER[c])
+                if c == WO_AFTER:
+                    load_wo_scales()
+                if c >= WO_AFTER:
+                    load_wo(c - WO_AFTER)
+            load_wo(NF - 1)
 
             for s in range(NS):
                 scale_x(s, nc.scalar)
                 scale_x(s, nc.vector)
                 turn_x(s)
-                if s in (1, 2):
-                    widen(s - 1)
+                if s % 2 == 1:
+                    widen(s // 2)
             copy_x(0)
             widen(2)
             copy_x(1)
-            turn_a(0)
-            weave(0, range(4))
-            weave(1, (0, 1))
+            turn_a(2, 0)
+            turn_a(2, 1)
+            weave(0, range(4), nc.vector)
+            weave(1, (0, 1), nc.vector)
             quantize_w(0)
-            weave(1, (2, 3))
+            weave(1, (2, 3), nc.vector)
             quantize_x(0)
-            multiply_z(0, (0,))
+            multiply_z(0, (0, 1))
             for c in range(NG, 1 + LEAD):
                 widen(c)
 
+            last = NC - 1
+            gates = [(0, 2, 1), (1, 0, 1), (1, 1, 1), (1, 2, 1), (0, 3, 1), (1, 3, 1)] + [(s, G, 1) for s in (2, 3) for G in range(4)]
             for c in range(1, NC):
                 G, g = divmod(c, NG)
+                for k in SW0.get(c, []):
+                    weave(k, range(4), nc.scalar)
+                if g == 0:
+                    sigmoid(G - 1)
                 for s, half in COPY_A.get(c, []):
                     copy_a(s, half)
-                if g == 0:
-                    for lo in (0, T // 2):
-                        sigmoid(G - 1, lo, T // 2)
-                if c in WIDEN:
-                    widen(WIDEN[c])
-                if c + 1 < NC:
-                    weave(c + 1, (0, 1))
+                for k in WIDEN.get(c, []):
+                    widen(k)
+                for k in SW.get(c, []):
+                    weave(k, range(4), nc.scalar)
+                if c < last:
+                    weave(c + 1, (0, 1), nc.vector)
                 if c - 1 in GATES:
-                    quantize_h(GATES[c - 1], 0)
-                quantize_w(c)
-                for G_done in ADD_Y.get(c, []):
-                    add_to_y(G_done, 0)
+                    quantize_h(0, GATES[c - 1], 1)
+                if c == last:
+                    gate(*gates[0])
+                quantize_w(c, 2 if c == last else 1)
+                for k, n in ADD_Y.get(c, []):
+                    multiply_y(k, 0, n)
                 if c == 1:
-                    multiply_z(1, (0,))
+                    multiply_z(1, (0, 1))
                     quantize_x(1)
-                    multiply_z(0, (1,))
-                    multiply_z(1, (1,))
-                else:
+                    multiply_z(0, (2, 3))
+                    multiply_z(1, (2, 3))
+                elif g == 0:
                     multiply_z(c, (0, 1))
-                for s in TURN_A.get(c, []):
-                    turn_a(s)
-                if c + 1 < NC:
-                    weave(c + 1, (2, 3))
+                elif g == 1:
+                    multiply_z(c, (0, 1))
+                    for i in (2, 3):
+                        multiply_z(c - 1, (i,))
+                        multiply_z(c, (i,))
+                else:
+                    multiply_z(c, range(Z_BANKS))
+                for s, half in TURN_A.get(c, []):
+                    turn_a(s, half)
+                if c < last:
+                    weave(c + 1, (2, 3), nc.vector)
                 if c in GATES:
-                    gate(GATES[c], 0)
+                    gate(0, GATES[c], 1)
 
-            for s in range(NS):
-                sigmoid(NF - 1, P * s, P)
-            rest = [(0, 1), (1, 1), (2, 1), (3, 0), (3, 1)] + [(G, s) for s in (2, 3) for G in range(NF)]
-            gate(*rest[0])
-            for i, done in enumerate(rest):
-                if i + 1 < len(rest):
-                    gate(*rest[i + 1])
-                quantize_h(*done)
-                add_to_y(*done)
+            sigmoid(NF - 1)
+            for i, (s, first, groups) in enumerate(gates):
+                if i + 1 < len(gates):
+                    gate(*gates[i + 1])
+                quantize_h(s, first, groups)
+                if s < NS - 1:
+                    for n in range(NN):
+                        for G in range(first, first + groups):
+                            multiply_y(G, s, n)
+                        if G == NF - 1:
+                            store_y(y[s, n][:], s, 512 * n, 512, nc.scalar)
+            s = NS - 1
+            for n in range(NN - 1):
+                for G in range(NF):
+                    multiply_y(G, s, n)
+                store_y(y[s, n][:], s, 512 * n, 512, nc.scalar)
+            lo = 512 * (NN - 1)
+            for width, i, engine in ((TAILA, OUT_BANKS[s][2], nc.vector), (512 - TAILA, TAIL_BANK, nc.scalar)):
+                piece = bank(i, "y")
+                for k in range(0, width, P):
+                    for G in range(NF):
+                        add_pass(piece[:, k : k + P], G, s, lo + k, P)
+                store_y(piece[:, :width], s, lo, width, engine)
+                lo += width

@@ -29,21 +29,21 @@ SCALE_BLOCK = 128
 HEADS = 16
 HALF = T // 2
 
-SCALAR_TILES = (0, 1, 3)
+SCALAR_TILES = (0, 1)
 LEAD = 4
 Z_BANKS = 4
 WO_AFTER = 9
 A_AFTER = {2: 2, 4: 3, 6: 0, 7: 1}
 A_BANKS = ((6, 7), (5, 4), (6, 7), (4, 5))
 A_IN_PSUM = ((0, 0), (1, 0))
-TURN_A = {2: [(3, 0), (3, 1)], 3: [(0, 0), (0, 1)], 4: [(1, 1), (1, 0)]}
-COPY_A = {2: [(2, 0), (2, 1)], 4: [(3, 0), (3, 1)], 5: [(0, 1), (1, 1)]}
+TURN_A = {2: [(3, 0), (3, 1)], 3: [(0, 0), (0, 1)], 5: [(1, 1), (1, 0)]}
+COPY_A = {2: [(2, 0), (2, 1)], 4: [(3, 0), (3, 1)], 7: [(0, 1), (1, 1)]}
 WIDEN = {1: [5], 2: [6], 3: [7], 4: [8], 5: [9], 6: [10], 7: [11]}
-SCALAR_WEAVES = {10: 2, 11: 1}
+SCALAR_WEAVES = {}
 SW0 = {8: [10]}
 SW = {9: [11]}
-GATES = {4: 0, 7: 1}
-ADD_Y = {7: [(0, 1), (0, 2)], 8: [(0, 0), (1, 0), (1, 1), (1, 2)]}
+GATES = {6: 0, 8: 1}
+ADD_Y = {8: [(0, 1), (0, 2)], 9: [(0, 0), (1, 0), (1, 1), (1, 2)]}
 TAILA = 256
 TAIL_BANK = 0
 OUT_BANKS = ((6, 7, 4), (5, 0, 1), (2, 3, 6), (7, 4, 5))

@@ -83,9 +83,9 @@ def tile_sigmoid_gated_attention_output_d4_kernel(
         ident = keep.tile([P, P], F32, name="ident")
         warm = keep.tile([P, 2], F32, name="warm")
 
-        nc.gpsimd.memset(warm[:], 0.0)
+        nc.vector.memset(warm[:], 0.0)
         make_identity(nc, ident[:])
-        nc.gpsimd.memset(wo_code_scales[:].rearrange("p g n -> p (g n)").bitcast(I32), 0)
+        nc.vector.memset(wo_code_scales[:].rearrange("p g n -> p (g n)").bitcast(I32), 0)
 
         w_bytes = {}
 

@@ -29,24 +29,21 @@ SCALE_BLOCK = 128
 HEADS = 16
 HALF = T // 2
 
-SCALAR_TILES = (0, 1)
+SCALAR_TILES = (0, 1, 2)
 LEAD = 4
+
 Z_BANKS = 4
-WO_AFTER = 9
-A_AFTER = {2: 2, 4: 3, 6: 0, 7: 1}
 A_BANKS = ((6, 7), (5, 4), (6, 7), (4, 5))
 A_IN_PSUM = ((0, 0), (1, 0))
+OUT_BANKS = ((6, 7, 4), (5, 0, 1), (2, 3, 6), (7, 4, 5))
+LAST_BANK = 0
+
+LOAD_A = {2: 2, 4: 3, 6: 0, 7: 1}
 TURN_A = {2: [(3, 0), (3, 1)], 3: [(0, 0), (0, 1)], 5: [(1, 1), (1, 0)]}
 COPY_A = {2: [(2, 0), (2, 1)], 4: [(3, 0), (3, 1)], 7: [(0, 1), (1, 1)]}
-WIDEN = {1: [5], 2: [6], 3: [7], 4: [8], 5: [9], 6: [10], 7: [11]}
-SCALAR_WEAVES = {}
-SW0 = {8: [10]}
-SW = {9: [11]}
-GATES = {6: 0, 8: 1}
-ADD_Y = {8: [(0, 1), (0, 2)], 9: [(0, 0), (1, 0), (1, 1), (1, 2)]}
-TAILA = 256
-TAIL_BANK = 0
-OUT_BANKS = ((6, 7, 4), (5, 0, 1), (2, 3, 6), (7, 4, 5))
+LOAD_WO = 9
+EARLY_GATES = {6: 0, 8: 1}
+EARLY_PASSES = {8: [(0, 1), (0, 2)], 9: [(0, 0), (1, 0), (1, 1), (1, 2)]}
 
 
 def tile_sigmoid_gated_attention_output_d4_kernel(
@@ -75,7 +72,7 @@ def tile_sigmoid_gated_attention_output_d4_kernel(
         wg_scale = keep.tile([P, NG, F // SCALE_BLOCK], F32, name="wg_scale", align_bytes=64)
         a_rows = keep_list(NS, [P, F], BF16, "a_rows")
         a_turned = keep_list(NS, [P, NF * SLOTS * P], BF16, "a_turned")
-        gate_values = keep.tile([P, NS, 2, NF * P, 2], F32, name="gate_values", align_bytes=64)
+        gate_values = keep_list(2 * NF, [P, 2, HALF, 2], F32, "gate_values")
         h_codes = keep_list(NS, [P, NF * P], U32, "h_codes")
         h_code_scales = keep_list(NS, [P, NF * P], U8, "h_code_scales")
         wo_codes = keep_list(NF, [P, 2 * D], U8, "wo_codes")
@@ -194,21 +191,21 @@ def tile_sigmoid_gated_attention_output_d4_kernel(
             w_wide[c] = stage.tile([P, SLOTS * 512], BF16, name="w_wide", tag="w_wide", bufs=6, align_bytes=64)
             nc.scalar.copy(out=w_wide[c][:], in_=w_bytes[c][:].bitcast(E4M3))
 
-        def weave(c, blocks, engine):
+        def weave(c, blocks):
             G, g = divmod(c, NG)
             if c not in w_words:
                 w_words[c] = stage.tile([P, SLOTS * 512], BF16, name="w_words", tag="w_words", bufs=4, align_bytes=64)
             dst = w_words[c][:].rearrange("p (t m j) -> p m j t", t=SLOTS, j=SLOTS)
             src = w_wide[c][:].rearrange("p (j m t) -> p m j t", j=SLOTS, t=SLOTS)
             for b in blocks:
-                if (b >= SLOTS - SCALAR_WEAVES.get(c, 0)) != (engine is nc.scalar):
-                    continue
                 rows = slice(32 * b, 32 * (b + 1))
-                scale = wg_scale[:, g, 4 * G + b : 4 * G + b + 1]
-                if engine is nc.scalar:
-                    nc.scalar.activation(out=dst[:, rows], in_=src[:, rows], func=COPY, scale=scale)
-                else:
-                    nc.vector.tensor_scalar(out=dst[:, rows], in0=src[:, rows], scalar1=scale, scalar2=None, op0=MULT)
+                nc.vector.tensor_scalar(
+                    out=dst[:, rows],
+                    in0=src[:, rows],
+                    scalar1=wg_scale[:, g, 4 * G + b : 4 * G + b + 1],
+                    scalar2=None,
+                    op0=MULT,
+                )
 
         def quantize_w(c, pieces=1):
             width = PASS // pieces
@@ -244,8 +241,8 @@ def tile_sigmoid_gated_attention_output_d4_kernel(
             for half in range(2):
                 for pair in range(2):
                     nc.scalar.activation(
-                        out=gate_values[:, 2 * half : 2 * half + 2, pair, P * G : P * (G + 1), :],
-                        in_=z[G, half, pair][:].rearrange("p (e i r) -> p i r e", e=2, i=2),
+                        out=gate_values[2 * G + half][:, pair],
+                        in_=z[G, half, pair][:].rearrange("p (e r) -> p r e", e=2),
                         func=SIGMOID,
                     )
 
@@ -265,22 +262,23 @@ def tile_sigmoid_gated_attention_output_d4_kernel(
 
         h_words, y = {}, {}
 
-        def gate(s, G, groups):
+        def gate(s, G):
             half, k = divmod(G, 2)
             if (s, half) in A_IN_PSUM:
                 a_values = a_banks[s, half][:].bitcast(BF16).rearrange("p (u r e) -> p r u e", u=2, e=2)
             else:
                 a_values = a_turned[s][:, 1024 * half : 1024 * (half + 1)].rearrange("p (r u e) -> p r u e", u=2, e=2)
-            h_words[s, G] = stage.tile([P, SLOTS * P * groups], BF16, name="h_words", tag="h_words", align_bytes=64)
+            sigmoids = gate_values[2 * G + s // 2][:].rearrange("p u r e -> p r u e")
+            h_words[s, G] = stage.tile([P, SLOTS * P], BF16, name="h_words", tag="h_words", align_bytes=64)
             nc.vector.tensor_tensor(
                 out=h_words[s, G][:].rearrange("p (r u e) -> p r u e", u=2, e=2),
-                in0=gate_values[:, s, :, P * G : P * (G + groups), :].rearrange("p u r e -> p r u e"),
-                in1=a_values[:, P * k : P * (k + groups)],
+                in0=sigmoids[:, P * (s % 2) : P * (s % 2 + 1)],
+                in1=a_values[:, P * k : P * (k + 1)],
                 op=MULT,
             )
 
-        def quantize_h(s, G, groups):
-            cols = slice(P * G, P * (G + groups))
+        def quantize_h(s, G):
+            cols = slice(P * G, P * (G + 1))
             nc.vector.quantize_mx(
                 out=h_codes[s][:, cols].bitcast(E4M3_X4), scales=h_code_scales[s][:, cols], in_=h_words[s, G][:]
             )
@@ -315,63 +313,62 @@ def tile_sigmoid_gated_attention_output_d4_kernel(
             nc.scalar.activation(out=warm[:, 1:2], in_=warm[:, 0:1], func=SIGMOID)
             load_x(0)
             load_x(1)
-            load_w(0)
             load_x(2)
+            load_w(0)
             load_x(3)
-            load_w(1)
             load_wg_scale()
+            load_w(1)
             for c in range(2, NC):
                 load_w(c)
-                if c in A_AFTER:
-                    load_a(A_AFTER[c])
-                if c == WO_AFTER:
+                if c in LOAD_A:
+                    load_a(LOAD_A[c])
+                if c == LOAD_WO:
                     load_wo_scales()
-                if c >= WO_AFTER:
-                    load_wo(c - WO_AFTER)
+                if c >= LOAD_WO:
+                    load_wo(c - LOAD_WO)
             load_wo(NF - 1)
 
             for s in range(NS):
                 scale_x(s, nc.scalar)
                 scale_x(s, nc.vector)
                 turn_x(s)
-                if s % 2 == 1:
-                    widen(s // 2)
+                if s >= 2:
+                    widen(s - 2)
             copy_x(0)
             widen(2)
             copy_x(1)
             turn_a(2, 0)
             turn_a(2, 1)
-            weave(0, range(4), nc.vector)
-            weave(1, (0, 1), nc.vector)
+            weave(0, range(4))
+            weave(1, (0, 1))
             quantize_w(0)
-            weave(1, (2, 3), nc.vector)
+            weave(1, (2, 3))
             quantize_x(0)
             multiply_z(0, (0, 1))
             for c in range(NG, 1 + LEAD):
                 widen(c)
 
+            gates = [(0, 2), (1, 0), (1, 1), (1, 2), (0, 3), (1, 3)] + [(s, G) for s in (2, 3) for G in range(NF)]
+
             last = NC - 1
-            gates = [(0, 2, 1), (1, 0, 1), (1, 1, 1), (1, 2, 1), (0, 3, 1), (1, 3, 1)] + [(s, G, 1) for s in (2, 3) for G in range(4)]
             for c in range(1, NC):
                 G, g = divmod(c, NG)
-                for k in SW0.get(c, []):
-                    weave(k, range(4), nc.scalar)
                 if g == 0:
                     sigmoid(G - 1)
                 for s, half in COPY_A.get(c, []):
                     copy_a(s, half)
-                for k in WIDEN.get(c, []):
-                    widen(k)
-                for k in SW.get(c, []):
-                    weave(k, range(4), nc.scalar)
+                if c + LEAD < NC:
+                    widen(c + LEAD)
                 if c < last:
-                    weave(c + 1, (0, 1), nc.vector)
-                if c - 1 in GATES:
-                    quantize_h(0, GATES[c - 1], 1)
+                    weave(c + 1, (0, 1))
+                if c - 1 in EARLY_GATES:
+                    quantize_h(0, EARLY_GATES[c - 1])
                 if c == last:
                     gate(*gates[0])
-                quantize_w(c, 2 if c == last else 1)
-                for k, n in ADD_Y.get(c, []):
+                    quantize_w(c, 2)
+                else:
+                    quantize_w(c)
+                for k, n in EARLY_PASSES.get(c, []):
                     multiply_y(k, 0, n)
                 if c == 1:
                     multiply_z(1, (0, 1))
@@ -390,31 +387,30 @@ def tile_sigmoid_gated_attention_output_d4_kernel(
                 for s, half in TURN_A.get(c, []):
                     turn_a(s, half)
                 if c < last:
-                    weave(c + 1, (2, 3), nc.vector)
-                if c in GATES:
-                    gate(0, GATES[c], 1)
+                    weave(c + 1, (2, 3))
+                if c in EARLY_GATES:
+                    gate(0, EARLY_GATES[c])
 
             sigmoid(NF - 1)
-            for i, (s, first, groups) in enumerate(gates):
+            last_tile = NS - 1
+            for i, (s, G) in enumerate(gates):
                 if i + 1 < len(gates):
                     gate(*gates[i + 1])
-                quantize_h(s, first, groups)
-                if s < NS - 1:
+                quantize_h(s, G)
+                if s < last_tile:
                     for n in range(NN):
-                        for G in range(first, first + groups):
-                            multiply_y(G, s, n)
+                        multiply_y(G, s, n)
                         if G == NF - 1:
                             store_y(y[s, n][:], s, 512 * n, 512, nc.scalar)
-            s = NS - 1
+
             for n in range(NN - 1):
                 for G in range(NF):
-                    multiply_y(G, s, n)
-                store_y(y[s, n][:], s, 512 * n, 512, nc.scalar)
-            lo = 512 * (NN - 1)
-            for width, i, engine in ((TAILA, OUT_BANKS[s][2], nc.vector), (512 - TAILA, TAIL_BANK, nc.scalar)):
+                    multiply_y(G, last_tile, n)
+                store_y(y[last_tile, n][:], last_tile, 512 * n, 512, nc.scalar)
+            for k, (i, engine) in enumerate(((OUT_BANKS[last_tile][NN - 1], nc.vector), (LAST_BANK, nc.scalar))):
+                lo = 512 * (NN - 1) + 256 * k
                 piece = bank(i, "y")
-                for k in range(0, width, P):
+                for col in (0, P):
                     for G in range(NF):
-                        add_pass(piece[:, k : k + P], G, s, lo + k, P)
-                store_y(piece[:, :width], s, lo, width, engine)
-                lo += width
+                        add_pass(piece[:, col : col + P], G, last_tile, lo + col, P)
+                store_y(piece[:, :256], last_tile, lo, 256, engine)

@@ -29,7 +29,7 @@ SCALE_BLOCK = 128
 HEADS = 16
 HALF = T // 2
 
-SCALAR_TILES = (0, 1, 2)
+SCALAR_TILES = (0, 1)
 LEAD = 4
 
 Z_BANKS = 4
@@ -43,7 +43,7 @@ TURN_A = {2: [(3, 0), (3, 1)], 3: [(0, 0), (0, 1)], 5: [(1, 1), (1, 0)]}
 COPY_A = {2: [(2, 0), (2, 1)], 4: [(3, 0), (3, 1)], 7: [(0, 1), (1, 1)]}
 LOAD_WO = 9
 EARLY_GATES = {6: 0, 8: 1}
-EARLY_PASSES = {8: [(0, 1), (0, 2)], 9: [(0, 0), (1, 0), (1, 1), (1, 2)]}
+EARLY_PASSES = {9: [(0, 1), (0, 2), (0, 0), (1, 0), (1, 1), (1, 2)]}
 
 
 def tile_sigmoid_gated_attention_output_d4_kernel(
@@ -207,6 +207,16 @@ def tile_sigmoid_gated_attention_output_d4_kernel(
                     op0=MULT,
                 )
 
+        def weave_on_scalar(c, b):
+            G, g = divmod(c, NG)
+            rows = slice(32 * b, 32 * (b + 1))
+            nc.scalar.activation(
+                out=w_words[c][:].rearrange("p (t m j) -> p m j t", t=SLOTS, j=SLOTS)[:, rows],
+                in_=w_wide[c][:].rearrange("p (j m t) -> p m j t", j=SLOTS, t=SLOTS)[:, rows],
+                func=COPY,
+                scale=wg_scale[:, g, 4 * G + b : 4 * G + b + 1],
+            )
+
         def quantize_w(c, pieces=1):
             width = PASS // pieces
             for lo in range(0, PASS, width):
@@ -313,11 +323,11 @@ def tile_sigmoid_gated_attention_output_d4_kernel(
             nc.scalar.activation(out=warm[:, 1:2], in_=warm[:, 0:1], func=SIGMOID)
             load_x(0)
             load_x(1)
-            load_x(2)
             load_w(0)
+            load_x(2)
             load_x(3)
-            load_wg_scale()
             load_w(1)
+            load_wg_scale()
             for c in range(2, NC):
                 load_w(c)
                 if c in LOAD_A:
@@ -332,8 +342,8 @@ def tile_sigmoid_gated_attention_output_d4_kernel(
                 scale_x(s, nc.scalar)
                 scale_x(s, nc.vector)
                 turn_x(s)
-                if s >= 2:
-                    widen(s - 2)
+                if s % 2 == 1:
+                    widen(s // 2)
             copy_x(0)
             widen(2)
             copy_x(1)
@@ -375,19 +385,15 @@ def tile_sigmoid_gated_attention_output_d4_kernel(
                     quantize_x(1)
                     multiply_z(0, (2, 3))
                     multiply_z(1, (2, 3))
-                elif g == 0:
-                    multiply_z(c, (0, 1))
-                elif g == 1:
-                    multiply_z(c, (0, 1))
-                    for i in (2, 3):
-                        multiply_z(c - 1, (i,))
-                        multiply_z(c, (i,))
                 else:
                     multiply_z(c, range(Z_BANKS))
                 for s, half in TURN_A.get(c, []):
                     turn_a(s, half)
-                if c < last:
+                if c < last - 1:
                     weave(c + 1, (2, 3))
+                elif c < last:
+                    weave(last, (2,))
+                    weave_on_scalar(last, 3)
                 if c in EARLY_GATES:
                     gate(0, EARLY_GATES[c])
 

@@ -35,8 +35,8 @@ LEAD = 4
 Z_BANKS = 4
 A_BANKS = ((6, 7), (5, 4), (6, 7), (4, 5))
 A_IN_PSUM = ((0, 0), (1, 0))
-OUT_BANKS = ((6, 7, 4), (5, 0, 1), (2, 3, 6), (7, 4, 5))
-LAST_BANK = 0
+OUT_BANKS = ((6, 7, 4), (5, 0, 1), (2, 3, 6), (7, 4))
+LAST_PIECES = ((5, 256), (0, 128), (1, 128))
 
 LOAD_A = {2: 2, 4: 3, 6: 0, 7: 1}
 TURN_A = {2: [(3, 0), (3, 1)], 3: [(0, 0), (0, 1)], 5: [(1, 1), (1, 0)]}
@@ -67,8 +67,8 @@ def tile_sigmoid_gated_attention_output_d4_kernel(
         x_codes = keep_list(NG, [P, T], U32, "x_codes")
         x_code_scales = keep_list(NG, [P, T], U8, "x_code_scales")
         x_scale = keep.tile([P, NS, D // SCALE_BLOCK], F32, name="x_scale", align_bytes=64)
-        w_codes = keep_list(NC, [P, PASS], U32, "w_codes")
-        w_code_scales = keep_list(NC, [P, PASS], U8, "w_code_scales")
+        w_codes = keep_list(NF, [P, NG * PASS], U32, "w_codes")
+        w_code_scales = keep_list(NF, [P, NG * PASS], U8, "w_code_scales")
         wg_scale = keep.tile([P, NG, F // SCALE_BLOCK], F32, name="wg_scale", align_bytes=64)
         a_rows = keep_list(NS, [P, F], BF16, "a_rows")
         a_turned = keep_list(NS, [P, NF * SLOTS * P], BF16, "a_turned")
@@ -193,9 +193,9 @@ def tile_sigmoid_gated_attention_output_d4_kernel(
 
         def weave(c, blocks):
             G, g = divmod(c, NG)
-            if c not in w_words:
-                w_words[c] = stage.tile([P, SLOTS * 512], BF16, name="w_words", tag="w_words", bufs=4, align_bytes=64)
-            dst = w_words[c][:].rearrange("p (t m j) -> p m j t", t=SLOTS, j=SLOTS)
+            if G not in w_words:
+                w_words[G] = stage.tile([P, NG * SLOTS * 512], BF16, name="w_words", tag="w_words", bufs=2, align_bytes=64)
+            dst = w_words[G][:, SLOTS * 512 * g : SLOTS * 512 * (g + 1)].rearrange("p (t m j) -> p m j t", t=SLOTS, j=SLOTS)
             src = w_wide[c][:].rearrange("p (j m t) -> p m j t", j=SLOTS, t=SLOTS)
             for b in blocks:
                 rows = slice(32 * b, 32 * (b + 1))
@@ -211,20 +211,18 @@ def tile_sigmoid_gated_attention_output_d4_kernel(
             G, g = divmod(c, NG)
             rows = slice(32 * b, 32 * (b + 1))
             nc.scalar.activation(
-                out=w_words[c][:].rearrange("p (t m j) -> p m j t", t=SLOTS, j=SLOTS)[:, rows],
+                out=w_words[G][:, SLOTS * 512 * g : SLOTS * 512 * (g + 1)].rearrange("p (t m j) -> p m j t", t=SLOTS, j=SLOTS)[:, rows],
                 in_=w_wide[c][:].rearrange("p (j m t) -> p m j t", j=SLOTS, t=SLOTS)[:, rows],
                 func=COPY,
                 scale=wg_scale[:, g, 4 * G + b : 4 * G + b + 1],
             )
 
-        def quantize_w(c, pieces=1):
-            width = PASS // pieces
-            for lo in range(0, PASS, width):
-                nc.vector.quantize_mx(
-                    out=w_codes[c][:, lo : lo + width].bitcast(E4M3_X4),
-                    scales=w_code_scales[c][:, lo : lo + width],
-                    in_=w_words[c][:, SLOTS * lo : SLOTS * (lo + width)],
-                )
+        def quantize_w(G, lo, width):
+            nc.vector.quantize_mx(
+                out=w_codes[G][:, lo : lo + width].bitcast(E4M3_X4),
+                scales=w_code_scales[G][:, lo : lo + width],
+                in_=w_words[G][:, SLOTS * lo : SLOTS * (lo + width)],
+            )
 
         z = {}
 
@@ -236,11 +234,11 @@ def tile_sigmoid_gated_attention_output_d4_kernel(
                 if g == 0:
                     z[G, half, pair] = bank(i, "z")
                 for e in range(2):
-                    cols = slice(P * (2 * pair + e), P * (2 * pair + e + 1))
+                    cols = slice(PASS * g + P * (2 * pair + e), PASS * g + P * (2 * pair + e + 1))
                     nc.tensor.matmul_mx(
                         out=z[G, half, pair][:, HALF * e : HALF * (e + 1)],
-                        lhsT=w_codes[c][:, cols].bitcast(E4M3_X4),
-                        lhsT_scale=w_code_scales[c][:, cols],
+                        lhsT=w_codes[G][:, cols].bitcast(E4M3_X4),
+                        lhsT_scale=w_code_scales[G][:, cols],
                         rhs=x_codes[g][:, tokens].bitcast(E4M3_X4),
                         rhs_scale=x_code_scales[g][:, tokens],
                         start=(g == 0 and e == 0),
@@ -350,11 +348,8 @@ def tile_sigmoid_gated_attention_output_d4_kernel(
             turn_a(2, 0)
             turn_a(2, 1)
             weave(0, range(4))
-            weave(1, (0, 1))
-            quantize_w(0)
-            weave(1, (2, 3))
+            weave(1, range(4))
             quantize_x(0)
-            multiply_z(0, (0, 1))
             for c in range(NG, 1 + LEAD):
                 widen(c)
 
@@ -375,18 +370,26 @@ def tile_sigmoid_gated_attention_output_d4_kernel(
                     quantize_h(0, EARLY_GATES[c - 1])
                 if c == last:
                     gate(*gates[0])
-                    quantize_w(c, 2)
-                else:
-                    quantize_w(c)
+                    quantize_w(G, PASS * g, PASS // 2)
+                    quantize_w(G, PASS * g + PASS // 2, PASS // 2)
+                elif G == NF - 1 or g == NG - 1:
+                    quantize_w(G, PASS * g, PASS)
+                elif g == 1:
+                    quantize_w(G, 0, 2 * PASS)
                 for k, n in EARLY_PASSES.get(c, []):
                     multiply_y(k, 0, n)
                 if c == 1:
+                    multiply_z(0, (0, 1))
                     multiply_z(1, (0, 1))
                     quantize_x(1)
                     multiply_z(0, (2, 3))
                     multiply_z(1, (2, 3))
-                else:
+                elif G == NF - 1 or g == NG - 1:
                     multiply_z(c, range(Z_BANKS))
+                elif g == 1:
+                    for i in range(Z_BANKS):
+                        multiply_z(c - 1, (i,))
+                        multiply_z(c, (i,))
                 for s, half in TURN_A.get(c, []):
                     turn_a(s, half)
                 if c < last - 1:
@@ -413,10 +416,11 @@ def tile_sigmoid_gated_attention_output_d4_kernel(
                 for G in range(NF):
                     multiply_y(G, last_tile, n)
                 store_y(y[last_tile, n][:], last_tile, 512 * n, 512, nc.scalar)
-            for k, (i, engine) in enumerate(((OUT_BANKS[last_tile][NN - 1], nc.vector), (LAST_BANK, nc.scalar))):
-                lo = 512 * (NN - 1) + 256 * k
+            lo = 512 * (NN - 1)
+            for k, (i, width) in enumerate(LAST_PIECES):
                 piece = bank(i, "y")
-                for col in (0, P):
+                for col in range(0, width, P):
                     for G in range(NF):
                         add_pass(piece[:, col : col + P], G, last_tile, lo + col, P)
-                store_y(piece[:, :256], last_tile, lo, 256, engine)
+                store_y(piece[:, :width], last_tile, lo, width, nc.scalar if k % 2 else nc.vector)
+                lo = lo + width

@@ -38,10 +38,9 @@ A_IN_PSUM = ((0, 0), (1, 0))
 OUT_BANKS = ((6, 7, 4), (5, 0, 1), (2, 3, 6), (7, 4))
 LAST_PIECES = ((5, 256), (0, 128), (1, 128))
 
-LOAD_A = {2: 2, 4: 3, 6: 0, 7: 1}
+LOAD_A = {3: (2,), 6: (3, 0), 9: (1,)}
 TURN_A = {2: [(3, 0), (3, 1)], 3: [(0, 0), (0, 1)], 5: [(1, 1), (1, 0)]}
 COPY_A = {2: [(2, 0), (2, 1)], 4: [(3, 0), (3, 1)], 7: [(0, 1), (1, 1)]}
-LOAD_WO = 9
 EARLY_GATES = {6: 0, 8: 1}
 EARLY_PASSES = {9: [(0, 1), (0, 2), (0, 0), (1, 0), (1, 1), (1, 2)]}
 
@@ -309,7 +308,10 @@ def tile_sigmoid_gated_attention_output_d4_kernel(
             )
 
         def store_y(src, s, lo, width, engine):
-            y_rows = stage.tile([P, width], F32, name="y_rows", tag="w_wide", bufs=6, align_bytes=64)
+            if width == 512:
+                y_rows = stage.tile([P, width], F32, name="y_rows", tag="w_wide", bufs=6, align_bytes=64)
+            else:
+                y_rows = stage.tile([P, width], F32, name="y_piece", tag="y_piece", bufs=len(LAST_PIECES), align_bytes=64)
             if engine is nc.scalar:
                 nc.scalar.copy(out=y_rows[:], in_=src)
             else:
@@ -324,32 +326,30 @@ def tile_sigmoid_gated_attention_output_d4_kernel(
             load_w(0)
             load_x(2)
             load_x(3)
-            load_w(1)
             load_wg_scale()
-            for c in range(2, NC):
+            for c in range(1, NC):
                 load_w(c)
-                if c in LOAD_A:
-                    load_a(LOAD_A[c])
-                if c == LOAD_WO:
-                    load_wo_scales()
-                if c >= LOAD_WO:
-                    load_wo(c - LOAD_WO)
-            load_wo(NF - 1)
+                for s in LOAD_A.get(c, ()):
+                    load_a(s)
+            load_wo_scales()
+            for G in range(NF):
+                load_wo(G)
 
             for s in range(NS):
                 scale_x(s, nc.scalar)
                 scale_x(s, nc.vector)
                 turn_x(s)
-                if s % 2 == 1:
-                    widen(s // 2)
-            copy_x(0)
+                if s == 1:
+                    widen(0)
+                    copy_x(0)
+            widen(1)
             widen(2)
             copy_x(1)
             turn_a(2, 0)
             turn_a(2, 1)
             weave(0, range(4))
-            weave(1, range(4))
             quantize_x(0)
+            weave(1, range(4))
             for c in range(NG, 1 + LEAD):
                 widen(c)
 

@@ -43,6 +43,7 @@ TURN_A = {2: [(3, 0), (3, 1)], 3: [(0, 0), (0, 1)], 5: [(1, 1), (1, 0)]}
 COPY_A = {2: [(2, 0), (2, 1)], 4: [(3, 0), (3, 1)], 7: [(0, 1), (1, 1)]}
 EARLY_GATES = {6: 0, 8: 1}
 EARLY_PASSES = {9: [(0, 1), (0, 2), (0, 0), (1, 0), (1, 1), (1, 2)]}
+MOVING_CODES, MOVING_SCALES, STATIONARY_CODES, STATIONARY_SCALES = 0, 128, 192, 64
 
 
 def tile_sigmoid_gated_attention_output_d4_kernel(
@@ -60,28 +61,33 @@ def tile_sigmoid_gated_attention_output_d4_kernel(
         def keep_list(count, shape, dtype, name):
             return [keep.tile(shape, dtype, name="%s%d" % (name, i), align_bytes=64) for i in range(count)]
 
+        def shifted_list(count, columns, dtype, size, shift, name):
+            tile = keep.tile([P, count * columns + shift // size], dtype, name=name, align_bytes=256)
+            return [tile[:, shift // size + columns * i : shift // size + columns * (i + 1)] for i in range(count)]
+
         x_bytes = keep_list(NS, [P, D], U8, "x_bytes")
         x_values = keep_list(NS, [P, D], BF16, "x_values")
         x_words = keep_list(NG, [P, SLOTS * T], BF16, "x_words")
-        x_codes = keep_list(NG, [P, T], U32, "x_codes")
-        x_code_scales = keep_list(NG, [P, T], U8, "x_code_scales")
+        x_codes = shifted_list(NG, T, U32, 4, MOVING_CODES, "x_codes")
+        x_code_scales = shifted_list(NG, T, U8, 1, MOVING_SCALES, "x_code_scales")
         x_scale = keep.tile([P, NS, D // SCALE_BLOCK], F32, name="x_scale", align_bytes=64)
-        w_codes = keep_list(NF, [P, NG * PASS], U32, "w_codes")
-        w_code_scales = keep_list(NF, [P, NG * PASS], U8, "w_code_scales")
+        w_codes = shifted_list(NF, NG * PASS, U32, 4, STATIONARY_CODES, "w_codes")
+        w_code_scales = shifted_list(NF, NG * PASS, U8, 1, STATIONARY_SCALES, "w_code_scales")
         wg_scale = keep.tile([P, NG, F // SCALE_BLOCK], F32, name="wg_scale", align_bytes=64)
         a_rows = keep_list(NS, [P, F], BF16, "a_rows")
         a_turned = keep_list(NS, [P, NF * SLOTS * P], BF16, "a_turned")
         gate_values = keep_list(2 * NF, [P, 2, HALF, 2], F32, "gate_values")
-        h_codes = keep_list(NS, [P, NF * P], U32, "h_codes")
-        h_code_scales = keep_list(NS, [P, NF * P], U8, "h_code_scales")
-        wo_codes = keep_list(NF, [P, 2 * D], U8, "wo_codes")
-        wo_code_scales = keep.tile([P, NF, D], U8, name="wo_code_scales", align_bytes=64)
+        h_codes = shifted_list(NS, NF * P, U32, 4, STATIONARY_CODES, "h_codes")
+        h_code_scales = shifted_list(NS, NF * P, U8, 1, STATIONARY_SCALES, "h_code_scales")
+        wo_codes = shifted_list(NF, 2 * D, U8, 1, MOVING_CODES, "wo_codes")
+        wo_scale_rows = shifted_list(1, NF * D, U8, 1, MOVING_SCALES, "wo_code_scales")[0]
+        wo_code_scales = wo_scale_rows.rearrange("p (g n) -> p g n", g=NF)
         ident = keep.tile([P, P], F32, name="ident")
         warm = keep.tile([P, 2], F32, name="warm")
 
         nc.vector.memset(warm[:], 0.0)
         make_identity(nc, ident[:])
-        nc.vector.memset(wo_code_scales[:].rearrange("p g n -> p (g n)").bitcast(I32), 0)
+        nc.vector.memset(wo_scale_rows.bitcast(I32), 0)
 
         w_bytes = {}
 
@@ -113,7 +119,7 @@ def tile_sigmoid_gated_attention_output_d4_kernel(
             )
 
         def load_wo(G):
-            nc.sync.dma_start(out=wo_codes[G][:], in_=Wo_words[G])
+            nc.sync.dma_start(out=wo_codes[G], in_=Wo_words[G])
 
         def load_wo_scales():
             for r in range(4):

@@ -25,25 +25,28 @@ NG = D // PASS
 NF = F // PASS
 NN = D // 512
 NC = NF * NG
+NQ = 2 * NF
 SCALE_BLOCK = 128
+BLOCKS = PASS // SCALE_BLOCK
 HEADS = 16
 HALF = T // 2
+PAIR = 2 * P
 
 SCALAR_TILES = (0, 1)
 LEAD = 4
+WIDE_BUFS = 6
+BYTE_BUFS = 8
 
-Z_BANKS = 4
-A_BANKS = ((6, 7), (5, 4), (6, 7), (4, 5))
-A_IN_PSUM = ((0, 0), (1, 0))
-OUT_BANKS = ((6, 7, 4), (5, 0, 1), (2, 3, 6), (7, 4))
-LAST_PIECES = ((5, 256), (0, 128), (1, 128))
+X_BANKS = ((0, 1, 2), (3, 4, 5))
+Z_BANKS = [(q % 2, 2 + q % 2) for q in range(NQ)]
+A_BANKS = ((6, 7), (4, 5), (6, 7), (4, 5))
+A_COPIED = (2, 3)
+OUT_BANKS = ((0, 2, 6), (1, 3, 4), (7, 5, 0), (2, 6))
+LAST_PIECES = ((1, 256), (3, 128), (4, 128))
 
 LOAD_A = {3: (2,), 6: (3, 0), 9: (1,)}
-TURN_A = {2: [(3, 0), (3, 1)], 3: [(0, 0), (0, 1)], 5: [(1, 1), (1, 0)]}
-COPY_A = {2: [(2, 0), (2, 1)], 4: [(3, 0), (3, 1)], 7: [(0, 1), (1, 1)]}
-EARLY_GATES = {6: 0, 8: 1}
-EARLY_PASSES = {9: [(0, 1), (0, 2), (0, 0), (1, 0), (1, 1), (1, 2)]}
-MOVING_CODES, MOVING_SCALES, STATIONARY_CODES, STATIONARY_SCALES = 0, 128, 192, 64
+TURN_A = {2: [(3, 0), (3, 1)], 3: [(0, 0)], 4: [(0, 1)], 5: [(1, 0), (1, 1)]}
+COPY_A = {2: [(2, 0), (2, 1)], 4: [(3, 0), (3, 1)]}
 
 
 def tile_sigmoid_gated_attention_output_d4_kernel(
@@ -61,33 +64,29 @@ def tile_sigmoid_gated_attention_output_d4_kernel(
         def keep_list(count, shape, dtype, name):
             return [keep.tile(shape, dtype, name="%s%d" % (name, i), align_bytes=64) for i in range(count)]
 
-        def shifted_list(count, columns, dtype, size, shift, name):
-            tile = keep.tile([P, count * columns + shift // size], dtype, name=name, align_bytes=256)
-            return [tile[:, shift // size + columns * i : shift // size + columns * (i + 1)] for i in range(count)]
-
         x_bytes = keep_list(NS, [P, D], U8, "x_bytes")
         x_values = keep_list(NS, [P, D], BF16, "x_values")
         x_words = keep_list(NG, [P, SLOTS * T], BF16, "x_words")
-        x_codes = shifted_list(NG, T, U32, 4, MOVING_CODES, "x_codes")
-        x_code_scales = shifted_list(NG, T, U8, 1, MOVING_SCALES, "x_code_scales")
+        x_codes = keep_list(NG, [P, T], U32, "x_codes")
+        x_code_scales = keep_list(NG, [P, T], U8, "x_code_scales")
         x_scale = keep.tile([P, NS, D // SCALE_BLOCK], F32, name="x_scale", align_bytes=64)
-        w_codes = shifted_list(NF, NG * PASS, U32, 4, STATIONARY_CODES, "w_codes")
-        w_code_scales = shifted_list(NF, NG * PASS, U8, 1, STATIONARY_SCALES, "w_code_scales")
+        w_codes = keep_list(NF, [P, NG * PASS], U32, "w_codes")
+        w_code_scales = keep_list(NF, [P, NG * PASS], U8, "w_code_scales")
         wg_scale = keep.tile([P, NG, F // SCALE_BLOCK], F32, name="wg_scale", align_bytes=64)
         a_rows = keep_list(NS, [P, F], BF16, "a_rows")
-        a_turned = keep_list(NS, [P, NF * SLOTS * P], BF16, "a_turned")
+        a_turned = {s: keep.tile([P, NF * SLOTS * P], BF16, name="a_turned%d" % s, align_bytes=64) for s in A_COPIED}
         gate_values = keep_list(2 * NF, [P, 2, HALF, 2], F32, "gate_values")
-        h_codes = shifted_list(NS, NF * P, U32, 4, STATIONARY_CODES, "h_codes")
-        h_code_scales = shifted_list(NS, NF * P, U8, 1, STATIONARY_SCALES, "h_code_scales")
-        wo_codes = shifted_list(NF, 2 * D, U8, 1, MOVING_CODES, "wo_codes")
-        wo_scale_rows = shifted_list(1, NF * D, U8, 1, MOVING_SCALES, "wo_code_scales")[0]
-        wo_code_scales = wo_scale_rows.rearrange("p (g n) -> p g n", g=NF)
+        h_codes = keep_list(NS, [P, NF * P], U32, "h_codes")
+        h_code_scales = keep_list(NS, [P, NF * P], U8, "h_code_scales")
+        wo_codes = keep_list(NF, [P, 2 * D], U8, "wo_codes")
+        wo_scale_rows = keep.tile([P, NF * D], U8, name="wo_code_scales", align_bytes=64)
+        wo_code_scales = wo_scale_rows[:].rearrange("p (g n) -> p g n", g=NF)
         ident = keep.tile([P, P], F32, name="ident")
         warm = keep.tile([P, 2], F32, name="warm")
 
         nc.vector.memset(warm[:], 0.0)
         make_identity(nc, ident[:])
-        nc.vector.memset(wo_scale_rows.bitcast(I32), 0)
+        nc.vector.memset(wo_scale_rows[:].bitcast(I32), 0)
 
         w_bytes = {}
 
@@ -99,17 +98,17 @@ def tile_sigmoid_gated_attention_output_d4_kernel(
 
         def load_w(c):
             G, g = divmod(c, NG)
-            w_bytes[c] = stage.tile([P, SLOTS * 512], U8, name="w_bytes", tag="w_bytes", bufs=8, align_bytes=64)
+            w_bytes[c] = stage.tile([P, SLOTS * 512], U8, name="w_bytes", tag="w_bytes", bufs=BYTE_BUFS, align_bytes=64)
             nc.sync.dma_start(
                 out=w_bytes[c][:].rearrange("p (j n) -> p j n", j=SLOTS),
                 in_=Wg_bytes[PASS * g : PASS * (g + 1), 512 * G : 512 * (G + 1)].rearrange("(p j) n -> p j n", j=SLOTS),
             )
 
         def load_wg_scale():
-            for q in range(4):
+            for r in range(4):
                 nc.sync.dma_start(
-                    out=wg_scale[32 * q : 32 * (q + 1), :, :],
-                    in_=Wg_scale.rearrange("(g q) b -> q g b", q=4)[q].partition_broadcast(32),
+                    out=wg_scale[32 * r : 32 * (r + 1), :, :],
+                    in_=Wg_scale.rearrange("(g r) b -> r g b", r=4)[r].partition_broadcast(32),
                 )
 
         def load_a(s):
@@ -119,7 +118,7 @@ def tile_sigmoid_gated_attention_output_d4_kernel(
             )
 
         def load_wo(G):
-            nc.sync.dma_start(out=wo_codes[G], in_=Wo_words[G])
+            nc.sync.dma_start(out=wo_codes[G][:], in_=Wo_words[G])
 
         def load_wo_scales():
             for r in range(4):
@@ -135,21 +134,21 @@ def tile_sigmoid_gated_attention_output_d4_kernel(
 
         def scale_x(s, engine):
             for j in range(D // SCALE_BLOCK):
-                g, q = divmod(j, SLOTS)
+                g, b = divmod(j, BLOCKS)
                 if on_scalar(s, g) != (engine is nc.scalar):
                     continue
                 codes = x_bytes[s][:, SCALE_BLOCK * j : SCALE_BLOCK * (j + 1)].bitcast(E4M3)
                 values = x_values[s][:, PASS * g : PASS * (g + 1)]
                 if engine is nc.scalar:
                     nc.scalar.activation(
-                        out=values[:, SCALE_BLOCK * q : SCALE_BLOCK * (q + 1)],
+                        out=values[:, SCALE_BLOCK * b : SCALE_BLOCK * (b + 1)],
                         in_=codes,
                         func=COPY,
                         scale=x_scale[:, s, j : j + 1],
                     )
                 else:
                     nc.vector.tensor_scalar(
-                        out=values.rearrange("p (u m e) -> p m u e", u=2, e=2)[:, 32 * q : 32 * (q + 1)],
+                        out=values.rearrange("p (u m e) -> p m u e", u=2, e=2)[:, 32 * b : 32 * (b + 1)],
                         in0=codes.rearrange("p (m u e) -> p m u e", u=2, e=2),
                         scalar1=x_scale[:, s, j : j + 1],
                         scalar2=None,
@@ -165,7 +164,7 @@ def tile_sigmoid_gated_attention_output_d4_kernel(
             half, i = divmod(s, 2)
             for g in range(NG):
                 if i == 0:
-                    x_turned[half, g] = bank(NG * half + g, "x_turned")
+                    x_turned[half, g] = bank(X_BANKS[half][g], "x_turned")
                 dst = [x_turned[half, g][:, 256 * u + P * i : 256 * u + P * (i + 1)] for u in range(2)]
                 if on_scalar(s, g):
                     transpose_words(dst, x_values[s][:], g)
@@ -193,10 +192,10 @@ def tile_sigmoid_gated_attention_output_d4_kernel(
         w_wide, w_words = {}, {}
 
         def widen(c):
-            w_wide[c] = stage.tile([P, SLOTS * 512], BF16, name="w_wide", tag="w_wide", bufs=6, align_bytes=64)
+            w_wide[c] = stage.tile([P, SLOTS * 512], BF16, name="w_wide", tag="w_wide", bufs=WIDE_BUFS, align_bytes=64)
             nc.scalar.copy(out=w_wide[c][:], in_=w_bytes[c][:].bitcast(E4M3))
 
-        def weave(c, blocks):
+        def weave(c, slots, blocks, engine):
             G, g = divmod(c, NG)
             if G not in w_words:
                 w_words[G] = stage.tile([P, NG * SLOTS * 512], BF16, name="w_words", tag="w_words", bufs=2, align_bytes=64)
@@ -204,23 +203,13 @@ def tile_sigmoid_gated_attention_output_d4_kernel(
             src = w_wide[c][:].rearrange("p (j m t) -> p m j t", j=SLOTS, t=SLOTS)
             for b in blocks:
                 rows = slice(32 * b, 32 * (b + 1))
-                nc.vector.tensor_scalar(
-                    out=dst[:, rows],
-                    in0=src[:, rows],
-                    scalar1=wg_scale[:, g, 4 * G + b : 4 * G + b + 1],
-                    scalar2=None,
-                    op0=MULT,
-                )
-
-        def weave_on_scalar(c, b):
-            G, g = divmod(c, NG)
-            rows = slice(32 * b, 32 * (b + 1))
-            nc.scalar.activation(
-                out=w_words[G][:, SLOTS * 512 * g : SLOTS * 512 * (g + 1)].rearrange("p (t m j) -> p m j t", t=SLOTS, j=SLOTS)[:, rows],
-                in_=w_wide[c][:].rearrange("p (j m t) -> p m j t", j=SLOTS, t=SLOTS)[:, rows],
-                func=COPY,
-                scale=wg_scale[:, g, 4 * G + b : 4 * G + b + 1],
-            )
+                scale = wg_scale[:, g, BLOCKS * G + b : BLOCKS * G + b + 1]
+                if engine is nc.scalar:
+                    nc.scalar.activation(out=dst[:, rows, :, slots], in_=src[:, rows, :, slots], func=COPY, scale=scale)
+                else:
+                    nc.vector.tensor_scalar(
+                        out=dst[:, rows, :, slots], in0=src[:, rows, :, slots], scalar1=scale, scalar2=None, op0=MULT
+                    )
 
         def quantize_w(G, lo, width):
             nc.vector.quantize_mx(
@@ -231,56 +220,53 @@ def tile_sigmoid_gated_attention_output_d4_kernel(
 
         z = {}
 
-        def multiply_z(c, banks):
-            G, g = divmod(c, NG)
-            for i in banks:
-                half, pair = divmod(i, 2)
-                tokens = slice(HALF * half, HALF * (half + 1))
-                if g == 0:
-                    z[G, half, pair] = bank(i, "z")
-                for e in range(2):
-                    cols = slice(PASS * g + P * (2 * pair + e), PASS * g + P * (2 * pair + e + 1))
-                    nc.tensor.matmul_mx(
-                        out=z[G, half, pair][:, HALF * e : HALF * (e + 1)],
-                        lhsT=w_codes[G][:, cols].bitcast(E4M3_X4),
-                        lhsT_scale=w_code_scales[G][:, cols],
-                        rhs=x_codes[g][:, tokens].bitcast(E4M3_X4),
-                        rhs_scale=x_code_scales[g][:, tokens],
-                        start=(g == 0 and e == 0),
-                        stop=(g == NG - 1 and e == 1),
-                    )
+        def multiply_z(q, g, half):
+            G, pair = divmod(q, 2)
+            tokens = slice(HALF * half, HALF * (half + 1))
+            if g == 0:
+                z[q, half] = bank(Z_BANKS[q][half], "z")
+            for e in range(2):
+                cols = slice(PASS * g + PAIR * pair + P * e, PASS * g + PAIR * pair + P * (e + 1))
+                nc.tensor.matmul_mx(
+                    out=z[q, half][:, HALF * e : HALF * (e + 1)],
+                    lhsT=w_codes[G][:, cols].bitcast(E4M3_X4),
+                    lhsT_scale=w_code_scales[G][:, cols],
+                    rhs=x_codes[g][:, tokens].bitcast(E4M3_X4),
+                    rhs_scale=x_code_scales[g][:, tokens],
+                    start=(g == 0 and e == 0),
+                    stop=(g == NG - 1 and e == 1),
+                )
 
-        def sigmoid(G):
-            for half in range(2):
-                for pair in range(2):
-                    nc.scalar.activation(
-                        out=gate_values[2 * G + half][:, pair],
-                        in_=z[G, half, pair][:].rearrange("p (e r) -> p r e", e=2),
-                        func=SIGMOID,
-                    )
+        def sigmoid(q, half):
+            G, pair = divmod(q, 2)
+            nc.scalar.activation(
+                out=gate_values[2 * G + half][:, pair],
+                in_=z[q, half][:].rearrange("p (e r) -> p r e", e=2),
+                func=SIGMOID,
+            )
 
         a_banks = {}
 
-        def turn_a(s, half):
-            a_banks[s, half] = bank(A_BANKS[s][half], "a_bank")
+        def turn_a(s, side):
+            a_banks[s, side] = bank(A_BANKS[s][side], "a_bank")
             for k in range(2):
-                dst = [a_banks[s, half][:, 256 * u + P * k : 256 * u + P * (k + 1)] for u in range(2)]
-                transpose_words(dst, a_rows[s][:], 2 * half + k)
+                dst = [a_banks[s, side][:, 256 * u + P * k : 256 * u + P * (k + 1)] for u in range(2)]
+                transpose_words(dst, a_rows[s][:], 2 * side + k)
 
-        def copy_a(s, half):
+        def copy_a(s, side):
             nc.scalar.copy(
-                out=a_turned[s][:, 1024 * half : 1024 * (half + 1)].bitcast(F32).rearrange("p (r u) -> p r u", u=2),
-                in_=a_banks[s, half][:].rearrange("p (u r) -> p r u", u=2),
+                out=a_turned[s][:, 1024 * side : 1024 * (side + 1)].bitcast(F32).rearrange("p (r u) -> p r u", u=2),
+                in_=a_banks[s, side][:].rearrange("p (u r) -> p r u", u=2),
             )
 
         h_words, y = {}, {}
 
         def gate(s, G):
-            half, k = divmod(G, 2)
-            if (s, half) in A_IN_PSUM:
-                a_values = a_banks[s, half][:].bitcast(BF16).rearrange("p (u r e) -> p r u e", u=2, e=2)
+            side, k = divmod(G, 2)
+            if s in A_COPIED:
+                a_values = a_turned[s][:, 1024 * side : 1024 * (side + 1)].rearrange("p (r u e) -> p r u e", u=2, e=2)
             else:
-                a_values = a_turned[s][:, 1024 * half : 1024 * (half + 1)].rearrange("p (r u e) -> p r u e", u=2, e=2)
+                a_values = a_banks[s, side][:].bitcast(BF16).rearrange("p (u r e) -> p r u e", u=2, e=2)
             sigmoids = gate_values[2 * G + s // 2][:].rearrange("p u r e -> p r u e")
             h_words[s, G] = stage.tile([P, SLOTS * P], BF16, name="h_words", tag="h_words", align_bytes=64)
             nc.vector.tensor_tensor(
@@ -315,7 +301,7 @@ def tile_sigmoid_gated_attention_output_d4_kernel(
 
         def store_y(src, s, lo, width, engine):
             if width == 512:
-                y_rows = stage.tile([P, width], F32, name="y_rows", tag="w_wide", bufs=6, align_bytes=64)
+                y_rows = stage.tile([P, width], F32, name="y_rows", tag="w_wide", bufs=WIDE_BUFS, align_bytes=64)
             else:
                 y_rows = stage.tile([P, width], F32, name="y_piece", tag="y_piece", bufs=len(LAST_PIECES), align_bytes=64)
             if engine is nc.scalar:
@@ -341,6 +327,8 @@ def tile_sigmoid_gated_attention_output_d4_kernel(
             for G in range(NF):
                 load_wo(G)
 
+            all_slots = slice(0, SLOTS)
+            pair_slots = [slice(0, 2), slice(2, 4)]
             for s in range(NS):
                 scale_x(s, nc.scalar)
                 scale_x(s, nc.vector)
@@ -353,65 +341,75 @@ def tile_sigmoid_gated_attention_output_d4_kernel(
             copy_x(1)
             turn_a(2, 0)
             turn_a(2, 1)
-            weave(0, range(4))
+            weave(0, all_slots, range(BLOCKS), nc.vector)
             quantize_x(0)
-            weave(1, range(4))
+            weave(1, all_slots, (0, 1), nc.vector)
+            quantize_w(0, 0, PASS)
+            multiply_z(0, 0, 0)
+            multiply_z(1, 0, 0)
+            weave(1, all_slots, (2, 3), nc.vector)
             for c in range(NG, 1 + LEAD):
                 widen(c)
 
-            gates = [(0, 2), (1, 0), (1, 1), (1, 2), (0, 3), (1, 3)] + [(s, G) for s in (2, 3) for G in range(NF)]
-
+            z_banks = [(pair, half) for half in range(2) for pair in range(2)]
             last = NC - 1
-            for c in range(1, NC):
+            for c in range(1, last - 1):
                 G, g = divmod(c, NG)
                 if g == 0:
-                    sigmoid(G - 1)
-                for s, half in COPY_A.get(c, []):
-                    copy_a(s, half)
+                    for pair, half in z_banks:
+                        sigmoid(2 * (G - 1) + pair, half)
+                for s, side in COPY_A.get(c, []):
+                    copy_a(s, side)
                 if c + LEAD < NC:
                     widen(c + LEAD)
-                if c < last:
-                    weave(c + 1, (0, 1))
-                if c - 1 in EARLY_GATES:
-                    quantize_h(0, EARLY_GATES[c - 1])
-                if c == last:
-                    gate(*gates[0])
-                    quantize_w(G, PASS * g, PASS // 2)
-                    quantize_w(G, PASS * g + PASS // 2, PASS // 2)
-                elif G == NF - 1 or g == NG - 1:
-                    quantize_w(G, PASS * g, PASS)
-                elif g == 1:
-                    quantize_w(G, 0, 2 * PASS)
-                for k, n in EARLY_PASSES.get(c, []):
-                    multiply_y(k, 0, n)
+                weave(c + 1, all_slots, (0, 1), nc.vector)
+                quantize_w(G, PASS * g, PASS)
                 if c == 1:
-                    multiply_z(0, (0, 1))
-                    multiply_z(1, (0, 1))
+                    passes = [(pair, 1, 0) for pair in range(2)]
+                    for pair, k, half in passes:
+                        multiply_z(pair, k, half)
                     quantize_x(1)
-                    multiply_z(0, (2, 3))
-                    multiply_z(1, (2, 3))
-                elif G == NF - 1 or g == NG - 1:
-                    multiply_z(c, range(Z_BANKS))
+                    passes = [(pair, k, 1) for pair in range(2) for k in range(2)]
+                elif g == 0:
+                    passes = [(pair, 0, half) for pair, half in z_banks[:-1]]
                 elif g == 1:
-                    for i in range(Z_BANKS):
-                        multiply_z(c - 1, (i,))
-                        multiply_z(c, (i,))
-                for s, half in TURN_A.get(c, []):
-                    turn_a(s, half)
-                if c < last - 1:
-                    weave(c + 1, (2, 3))
-                elif c < last:
-                    weave(last, (2,))
-                    weave_on_scalar(last, 3)
-                if c in EARLY_GATES:
-                    gate(0, EARLY_GATES[c])
+                    passes = [(pair, 1, half) for pair, half in z_banks[:-1]] + [(1, 0, 1), (1, 1, 1)]
+                else:
+                    passes = [(pair, g, half) for pair, half in z_banks]
+                for pair, k, half in passes:
+                    multiply_z(2 * G + pair, k, half)
+                for s, side in TURN_A.get(c, []):
+                    turn_a(s, side)
+                weave(c + 1, all_slots, (2, 3), nc.vector)
 
-            sigmoid(NF - 1)
+            gates = [(s, G) for s in (0, 1) for G in range(NF - 1)] + [(0, NF - 1), (1, NF - 1)]
+            gates = gates + [(s, G) for s in (2, 3) for G in range(NF)]
+
+            G, first, second = NF - 1, NQ - 2, NQ - 1
+            weave(last, pair_slots[1], range(BLOCKS), nc.scalar)
+            weave(last, pair_slots[0], (0, 1), nc.vector)
+            quantize_w(G, PASS, PAIR)
+            weave(last, pair_slots[0], (2, 3), nc.vector)
+            quantize_w(G, PASS + PAIR, PAIR)
+            quantize_w(G, 2 * PASS, PAIR)
+            gate(*gates[0])
+            quantize_w(G, 2 * PASS + PAIR, PAIR)
+            for q, k, half in [(first, 1, 0), (first, 1, 1), (second, 0, 1), (first, 2, 0), (first, 2, 1)]:
+                multiply_z(q, k, half)
+            for k in (1, 2):
+                for half in range(2):
+                    multiply_z(second, k, half)
+            for q in (first, second):
+                for half in range(2):
+                    sigmoid(q, half)
+
             last_tile = NS - 1
             for i, (s, G) in enumerate(gates):
-                if i + 1 < len(gates):
+                if 0 < i < len(gates) - 1:
                     gate(*gates[i + 1])
                 quantize_h(s, G)
+                if i == 0:
+                    gate(*gates[1])
                 if s < last_tile:
                     for n in range(NN):
                         multiply_y(G, s, n)

@@ -41,8 +41,8 @@ X_BANKS = ((0, 1, 2), (3, 4, 5))
 Z_BANKS = [(q % 2, 2 + q % 2) for q in range(NQ)]
 A_BANKS = ((6, 7), (4, 5), (6, 7), (4, 5))
 A_COPIED = (2, 3)
-OUT_BANKS = ((0, 2, 6), (1, 3, 4), (7, 5, 0), (2, 6))
-LAST_PIECES = ((1, 256), (3, 128), (4, 128))
+OUT_BANKS = ((0, 2, 6), (1, 3, 4), (7, 5, 0), (2,))
+LAST_PIECES = ((6, 256), (1, 256), (3, 256), (4, 128), (7, 128))
 
 LOAD_A = {3: (2,), 6: (3, 0), 9: (1,)}
 TURN_A = {2: [(3, 0), (3, 1)], 3: [(0, 0)], 4: [(0, 1)], 5: [(1, 0), (1, 1)]}
@@ -416,15 +416,13 @@ def tile_sigmoid_gated_attention_output_d4_kernel(
                         if G == NF - 1:
                             store_y(y[s, n][:], s, 512 * n, 512, nc.scalar)
 
-            for n in range(NN - 1):
-                for G in range(NF):
-                    multiply_y(G, last_tile, n)
-                store_y(y[last_tile, n][:], last_tile, 512 * n, 512, nc.scalar)
-            lo = 512 * (NN - 1)
+            for G in range(NF):
+                multiply_y(G, last_tile, 0)
+            store_y(y[last_tile, 0][:], last_tile, 0, 512, nc.scalar)
+            lo = 512
             for k, (i, width) in enumerate(LAST_PIECES):
                 piece = bank(i, "y")
-                for col in range(0, width, P):
-                    for G in range(NF):
-                        add_pass(piece[:, col : col + P], G, last_tile, lo + col, P)
+                for G in range(NF):
+                    add_pass(piece[:, :width], G, last_tile, lo, width)
                 store_y(piece[:, :width], last_tile, lo, width, nc.scalar if k % 2 else nc.vector)
                 lo = lo + width

@@ -41,8 +41,8 @@ X_BANKS = ((0, 1, 2), (3, 4, 5))
 Z_BANKS = [(q % 2, 2 + q % 2) for q in range(NQ)]
 A_BANKS = ((6, 7), (4, 5), (6, 7), (4, 5))
 A_COPIED = (2, 3)
-OUT_BANKS = ((0, 2, 6), (1, 3, 4), (7, 5, 0), (2,))
-LAST_PIECES = ((6, 256), (1, 256), (3, 256), (4, 128), (7, 128))
+OUT_BANKS = ((0, 6, 2), (1, 3, 7), (4, 5, 0), (2,))
+LAST_PIECES = ((6, 256), (1, 256), (3, 256), (7, 128), (4, 128))
 
 LOAD_A = {3: (2,), 6: (3, 0), 9: (1,)}
 TURN_A = {2: [(3, 0), (3, 1)], 3: [(0, 0)], 4: [(0, 1)], 5: [(1, 0), (1, 1)]}
@@ -382,7 +382,7 @@ def tile_sigmoid_gated_attention_output_d4_kernel(
                     turn_a(s, side)
                 weave(c + 1, all_slots, (2, 3), nc.vector)
 
-            gates = [(s, G) for s in (0, 1) for G in range(NF - 1)] + [(0, NF - 1), (1, NF - 1)]
+            gates = [(0, 0), (0, 1), (0, 2), (1, 0), (0, 3), (1, 1), (1, 2), (1, 3)]
             gates = gates + [(s, G) for s in (2, 3) for G in range(NF)]
 
             G, first, second = NF - 1, NQ - 2, NQ - 1
@@ -410,11 +410,14 @@ def tile_sigmoid_gated_attention_output_d4_kernel(
                 quantize_h(s, G)
                 if i == 0:
                     gate(*gates[1])
-                if s < last_tile:
-                    for n in range(NN):
-                        multiply_y(G, s, n)
-                        if G == NF - 1:
-                            store_y(y[s, n][:], s, 512 * n, 512, nc.scalar)
+                if s == last_tile or (s, G) == (last_tile - 1, NF - 2):
+                    continue
+                groups = (G - 1, G) if (s, G) == (last_tile - 1, NF - 1) else (G,)
+                for n in range(NN):
+                    for k in groups:
+                        multiply_y(k, s, n)
+                    if G == NF - 1:
+                        store_y(y[s, n][:], s, 512 * n, 512, nc.scalar)
 
             for G in range(NF):
                 multiply_y(G, last_tile, 0)

@@ -96,13 +96,12 @@ def tile_sigmoid_gated_attention_output_d4_kernel(
         def load_x(s):
             nc.sync.dma_start(out=x_bytes[s][:], in_=X_bytes.rearrange("(p s) k -> s p k", s=NS)[s])
 
-        def load_w(c):
+        def load_w(c, rows=slice(0, SLOTS)):
             G, g = divmod(c, NG)
-            w_bytes[c] = stage.tile([P, SLOTS * 512], U8, name="w_bytes", tag="w_bytes", bufs=BYTE_BUFS, align_bytes=64)
-            nc.sync.dma_start(
-                out=w_bytes[c][:].rearrange("p (j n) -> p j n", j=SLOTS),
-                in_=Wg_bytes[PASS * g : PASS * (g + 1), 512 * G : 512 * (G + 1)].rearrange("(p j) n -> p j n", j=SLOTS),
-            )
+            if c not in w_bytes:
+                w_bytes[c] = stage.tile([P, SLOTS * 512], U8, name="w_bytes", tag="w_bytes", bufs=BYTE_BUFS, align_bytes=64)
+            chunk = Wg_bytes[PASS * g : PASS * (g + 1), 512 * G : 512 * (G + 1)].rearrange("(p j) n -> p j n", j=SLOTS)
+            nc.sync.dma_start(out=w_bytes[c][:].rearrange("p (j n) -> p j n", j=SLOTS)[:, rows], in_=chunk[:, rows])
 
         def load_wg_scale():
             for r in range(4):
@@ -191,9 +190,11 @@ def tile_sigmoid_gated_attention_output_d4_kernel(
 
         w_wide, w_words = {}, {}
 
-        def widen(c):
-            w_wide[c] = stage.tile([P, SLOTS * 512], BF16, name="w_wide", tag="w_wide", bufs=WIDE_BUFS, align_bytes=64)
-            nc.scalar.copy(out=w_wide[c][:], in_=w_bytes[c][:].bitcast(E4M3))
+        def widen(c, rows=slice(0, SLOTS)):
+            if c not in w_wide:
+                w_wide[c] = stage.tile([P, SLOTS * 512], BF16, name="w_wide", tag="w_wide", bufs=WIDE_BUFS, align_bytes=64)
+            cols = slice(512 * rows.start, 512 * rows.stop)
+            nc.scalar.copy(out=w_wide[c][:, cols], in_=w_bytes[c][:, cols].bitcast(E4M3))
 
         def weave(c, slots, blocks, engine):
             G, g = divmod(c, NG)
@@ -315,8 +316,10 @@ def tile_sigmoid_gated_attention_output_d4_kernel(
             nc.scalar.activation(out=warm[:, 1:2], in_=warm[:, 0:1], func=SIGMOID)
             load_x(0)
             load_x(1)
-            load_w(0)
+            row_halves = (slice(0, 2), slice(2, 4))
+            load_w(0, row_halves[0])
             load_x(2)
+            load_w(0, row_halves[1])
             load_x(3)
             load_wg_scale()
             for c in range(1, NC):
@@ -334,7 +337,8 @@ def tile_sigmoid_gated_attention_output_d4_kernel(
                 scale_x(s, nc.vector)
                 turn_x(s)
                 if s == 1:
-                    widen(0)
+                    for rows in row_halves:
+                        widen(0, rows)
                     copy_x(0)
             widen(1)
             widen(2)
@@ -356,7 +360,7 @@ def tile_sigmoid_gated_attention_output_d4_kernel(
             for c in range(1, last - 1):
                 G, g = divmod(c, NG)
                 if g == 0:
-                    for pair, half in z_banks:
+                    for pair, half in z_banks if G < NF - 1 else z_banks[:-1]:
                         sigmoid(2 * (G - 1) + pair, half)
                 for s, side in COPY_A.get(c, []):
                     copy_a(s, side)
@@ -387,6 +391,7 @@ def tile_sigmoid_gated_attention_output_d4_kernel(
 
             G, first, second = NF - 1, NQ - 2, NQ - 1
             weave(last, pair_slots[1], range(BLOCKS), nc.scalar)
+            sigmoid(first - 1, 1)
             weave(last, pair_slots[0], (0, 1), nc.vector)
             quantize_w(G, PASS, PAIR)
             weave(last, pair_slots[0], (2, 3), nc.vector)
@@ -394,11 +399,10 @@ def tile_sigmoid_gated_attention_output_d4_kernel(
             quantize_w(G, 2 * PASS, PAIR)
             gate(*gates[0])
             quantize_w(G, 2 * PASS + PAIR, PAIR)
-            for q, k, half in [(first, 1, 0), (first, 1, 1), (second, 0, 1), (first, 2, 0), (first, 2, 1)]:
+            for q, k, half in [(first, 1, 0), (first, 1, 1), (second, 1, 0), (first, 2, 0), (first, 2, 1)]:
                 multiply_z(q, k, half)
-            for k in (1, 2):
-                for half in range(2):
-                    multiply_z(second, k, half)
+            for k, half in [(0, 1), (1, 1), (2, 0), (2, 1)]:
+                multiply_z(second, k, half)
             for q in (first, second):
                 for half in range(2):
                     sigmoid(q, half)

from contextlib import ExitStack

import concourse.mybir as mybir
from concourse.masks import make_identity

F32 = mybir.dt.float32
BF16 = mybir.dt.bfloat16
U32 = mybir.dt.uint32
I32 = mybir.dt.int32
U8 = mybir.dt.uint8
E4M3 = mybir.dt.float8_e4m3fn
E4M3_X4 = mybir.dt.float8_e4m3fn_x4
E2M1_X4 = mybir.dt.float4_e2m1fn_x4
MULT = mybir.AluOpType.mult
COPY = mybir.ActivationFunctionType.Copy
SIGMOID = mybir.ActivationFunctionType.Sigmoid

P = 128
T, D, F = 512, 1536, 2048
FLOPS = 2 * 2 * T * D * F
SLOTS = 4
PASS = P * SLOTS
NS = T // P
NG = D // PASS
NF = F // PASS
NN = D // 512
NC = NF * NG
NQ = 2 * NF
SCALE_BLOCK = 128
BLOCKS = PASS // SCALE_BLOCK
HEADS = 16
HALF = T // 2
PAIR = 2 * P

SCALAR_TILES = (0, 1)
LEAD = 4
WIDE_BUFS = 6
BYTE_BUFS = 8

X_BANKS = ((0, 1, 2), (3, 4, 5))
Z_BANKS = [(q % 2, 2 + q % 2) for q in range(NQ)]
A_BANKS = ((6, 7), (4, 5), (6, 7), (4, 5))
A_COPIED = (2, 3)
OUT_BANKS = ((0, 6, 2), (1, 3, 7), (4, 5, 0), (2,))
LAST_PIECES = ((6, 256), (1, 256), (3, 256), (7, 128), (4, 128))

LOAD_A = {3: (2,), 6: (3, 0), 9: (1,)}
TURN_A = {2: [(3, 0), (3, 1)], 3: [(0, 0)], 4: [(0, 1)], 5: [(1, 0), (1, 1)]}
COPY_A = {2: [(2, 0), (2, 1)], 4: [(3, 0), (3, 1)]}


def tile_sigmoid_gated_attention_output_d4_kernel(
    tc, X_bytes, X_scale, Wg_bytes, Wg_scale, A, Wo_words, Wo_scales, out
):
    nc = tc.nc
    with ExitStack() as ctx:
        keep = ctx.enter_context(tc.tile_pool(name="keep", bufs=1))
        stage = ctx.enter_context(tc.tile_pool(name="stage", bufs=3))
        psum = ctx.enter_context(tc.psum_pool(name="psum", bufs=1))

        def bank(i, name):
            return psum.tile([P, 512], F32, name=name, tag="bank%d" % i)

        def keep_list(count, shape, dtype, name):
            return [keep.tile(shape, dtype, name="%s%d" % (name, i), align_bytes=64) for i in range(count)]

        x_bytes = keep_list(NS, [P, D], U8, "x_bytes")
        x_values = keep_list(NS, [P, D], BF16, "x_values")
        x_words = keep_list(NG, [P, SLOTS * T], BF16, "x_words")
        x_codes = keep_list(NG, [P, T], U32, "x_codes")
        x_code_scales = keep_list(NG, [P, T], U8, "x_code_scales")
        x_scale = keep.tile([P, NS, D // SCALE_BLOCK], F32, name="x_scale", align_bytes=64)
        w_codes = keep_list(NF, [P, NG * PASS], U32, "w_codes")
        w_code_scales = keep_list(NF, [P, NG * PASS], U8, "w_code_scales")
        wg_scale = keep.tile([P, NG, F // SCALE_BLOCK], F32, name="wg_scale", align_bytes=64)
        a_rows = keep_list(NS, [P, F], BF16, "a_rows")
        a_turned = {s: keep.tile([P, NF * SLOTS * P], BF16, name="a_turned%d" % s, align_bytes=64) for s in A_COPIED}
        gate_values = keep_list(2 * NF, [P, 2, HALF, 2], F32, "gate_values")
        h_codes = keep_list(NS, [P, NF * P], U32, "h_codes")
        h_code_scales = keep_list(NS, [P, NF * P], U8, "h_code_scales")
        wo_codes = keep_list(NF, [P, 2 * D], U8, "wo_codes")
        wo_scale_rows = keep.tile([P, NF * D], U8, name="wo_code_scales", align_bytes=64)
        wo_code_scales = wo_scale_rows[:].rearrange("p (g n) -> p g n", g=NF)
        ident = keep.tile([P, P], F32, name="ident")
        warm = keep.tile([P, 2], F32, name="warm")

        nc.vector.memset(warm[:], 0.0)
        make_identity(nc, ident[:])
        nc.vector.memset(wo_scale_rows[:].bitcast(I32), 0)

        w_bytes = {}

        def load_x_scale():
            nc.scalar.dma_start(out=x_scale[:], in_=X_scale.rearrange("(p s) j -> p s j", s=NS))

        def load_x(s):
            nc.sync.dma_start(out=x_bytes[s][:], in_=X_bytes.rearrange("(p s) k -> s p k", s=NS)[s])

        def load_w(c, rows=slice(0, SLOTS)):
            G, g = divmod(c, NG)
            if c not in w_bytes:
                w_bytes[c] = stage.tile([P, SLOTS * 512], U8, name="w_bytes", tag="w_bytes", bufs=BYTE_BUFS, align_bytes=64)
            chunk = Wg_bytes[PASS * g : PASS * (g + 1), 512 * G : 512 * (G + 1)].rearrange("(p j) n -> p j n", j=SLOTS)
            nc.sync.dma_start(out=w_bytes[c][:].rearrange("p (j n) -> p j n", j=SLOTS)[:, rows], in_=chunk[:, rows])

        def load_wg_scale():
            for r in range(4):
                nc.sync.dma_start(
                    out=wg_scale[32 * r : 32 * (r + 1), :, :],
                    in_=Wg_scale.rearrange("(g r) b -> r g b", r=4)[r].partition_broadcast(32),
                )

        def load_a(s):
            nc.sync.dma_start(
                out=a_rows[s][:].rearrange("p (c e) -> p c e", c=HEADS),
                in_=A.rearrange("c (p s) e -> s p c e", s=NS)[s],
            )

        def load_wo(G):
            nc.sync.dma_start(out=wo_codes[G][:], in_=Wo_words[G])

        def load_wo_scales():
            for r in range(4):
                nc.sync.dma_start(
                    out=wo_code_scales[r:P:32, :, :].bitcast(I32),
                    in_=Wo_scales.rearrange("g (q r) n -> r q g n", r=4)[r].bitcast(I32),
                )

        x_turned = {}

        def on_scalar(s, g):
            return s in SCALAR_TILES and g == NG - 1

        def scale_x(s, engine):
            for j in range(D // SCALE_BLOCK):
                g, b = divmod(j, BLOCKS)
                if on_scalar(s, g) != (engine is nc.scalar):
                    continue
                codes = x_bytes[s][:, SCALE_BLOCK * j : SCALE_BLOCK * (j + 1)].bitcast(E4M3)
                values = x_values[s][:, PASS * g : PASS * (g + 1)]
                if engine is nc.scalar:
                    nc.scalar.activation(
                        out=values[:, SCALE_BLOCK * b : SCALE_BLOCK * (b + 1)],
                        in_=codes,
                        func=COPY,
                        scale=x_scale[:, s, j : j + 1],
                    )
                else:
                    nc.vector.tensor_scalar(
                        out=values.rearrange("p (u m e) -> p m u e", u=2, e=2)[:, 32 * b : 32 * (b + 1)],
                        in0=codes.rearrange("p (m u e) -> p m u e", u=2, e=2),
                        scalar1=x_scale[:, s, j : j + 1],
                        scalar2=None,
                        op0=MULT,
                    )

        def transpose_words(dst, rows, group):
            words = rows.bitcast(F32)
            for u in range(2):
                nc.tensor.transpose(dst[u], words[:, 256 * group + u : 256 * (group + 1) : 2], ident[:])

        def turn_x(s):
            half, i = divmod(s, 2)
            for g in range(NG):
                if i == 0:
                    x_turned[half, g] = bank(X_BANKS[half][g], "x_turned")
                dst = [x_turned[half, g][:, 256 * u + P * i : 256 * u + P * (i + 1)] for u in range(2)]
                if on_scalar(s, g):
                    transpose_words(dst, x_values[s][:], g)
                else:
                    words = x_values[s][:].bitcast(F32)
                    for u in range(2):
                        nc.tensor.transpose(dst[u], words[:, 256 * g + P * u : 256 * g + P * (u + 1)], ident[:])

        def copy_x(half):
            for g in range(NG):
                nc.scalar.copy(
                    out=x_words[g][:, 1024 * half : 1024 * (half + 1)].bitcast(F32).rearrange("p (r u) -> p r u", u=2),
                    in_=x_turned[half, g][:].rearrange("p (u r) -> p r u", u=2),
                )

        def quantize_x(half):
            for g in range(NG):
                cols = slice(256 * half, 256 * (half + 1))
                nc.vector.quantize_mx(
                    out=x_codes[g][:, cols].bitcast(E4M3_X4),
                    scales=x_code_scales[g][:, cols],
                    in_=x_words[g][:, 1024 * half : 1024 * (half + 1)],
                )

        w_wide, w_words = {}, {}

        def widen(c, rows=slice(0, SLOTS)):
            if c not in w_wide:
                w_wide[c] = stage.tile([P, SLOTS * 512], BF16, name="w_wide", tag="w_wide", bufs=WIDE_BUFS, align_bytes=64)
            cols = slice(512 * rows.start, 512 * rows.stop)
            nc.scalar.copy(out=w_wide[c][:, cols], in_=w_bytes[c][:, cols].bitcast(E4M3))

        def weave(c, slots, blocks, engine):
            G, g = divmod(c, NG)
            if G not in w_words:
                w_words[G] = stage.tile([P, NG * SLOTS * 512], BF16, name="w_words", tag="w_words", bufs=2, align_bytes=64)
            dst = w_words[G][:, SLOTS * 512 * g : SLOTS * 512 * (g + 1)].rearrange("p (t m j) -> p m j t", t=SLOTS, j=SLOTS)
            src = w_wide[c][:].rearrange("p (j m t) -> p m j t", j=SLOTS, t=SLOTS)
            for b in blocks:
                rows = slice(32 * b, 32 * (b + 1))
                scale = wg_scale[:, g, BLOCKS * G + b : BLOCKS * G + b + 1]
                if engine is nc.scalar:
                    nc.scalar.activation(out=dst[:, rows, :, slots], in_=src[:, rows, :, slots], func=COPY, scale=scale)
                else:
                    nc.vector.tensor_scalar(
                        out=dst[:, rows, :, slots], in0=src[:, rows, :, slots], scalar1=scale, scalar2=None, op0=MULT
                    )

        def quantize_w(G, lo, width):
            nc.vector.quantize_mx(
                out=w_codes[G][:, lo : lo + width].bitcast(E4M3_X4),
                scales=w_code_scales[G][:, lo : lo + width],
                in_=w_words[G][:, SLOTS * lo : SLOTS * (lo + width)],
            )

        z = {}

        def multiply_z(q, g, half):
            G, pair = divmod(q, 2)
            tokens = slice(HALF * half, HALF * (half + 1))
            if g == 0:
                z[q, half] = bank(Z_BANKS[q][half], "z")
            for e in range(2):
                cols = slice(PASS * g + PAIR * pair + P * e, PASS * g + PAIR * pair + P * (e + 1))
                nc.tensor.matmul_mx(
                    out=z[q, half][:, HALF * e : HALF * (e + 1)],
                    lhsT=w_codes[G][:, cols].bitcast(E4M3_X4),
                    lhsT_scale=w_code_scales[G][:, cols],
                    rhs=x_codes[g][:, tokens].bitcast(E4M3_X4),
                    rhs_scale=x_code_scales[g][:, tokens],
                    start=(g == 0 and e == 0),
                    stop=(g == NG - 1 and e == 1),
                )

        def sigmoid(q, half):
            G, pair = divmod(q, 2)
            nc.scalar.activation(
                out=gate_values[2 * G + half][:, pair],
                in_=z[q, half][:].rearrange("p (e r) -> p r e", e=2),
                func=SIGMOID,
            )

        a_banks = {}

        def turn_a(s, side):
            a_banks[s, side] = bank(A_BANKS[s][side], "a_bank")
            for k in range(2):
                dst = [a_banks[s, side][:, 256 * u + P * k : 256 * u + P * (k + 1)] for u in range(2)]
                transpose_words(dst, a_rows[s][:], 2 * side + k)

        def copy_a(s, side):
            nc.scalar.copy(
                out=a_turned[s][:, 1024 * side : 1024 * (side + 1)].bitcast(F32).rearrange("p (r u) -> p r u", u=2),
                in_=a_banks[s, side][:].rearrange("p (u r) -> p r u", u=2),
            )

        h_words, y = {}, {}

        def gate(s, G):
            side, k = divmod(G, 2)
            if s in A_COPIED:
                a_values = a_turned[s][:, 1024 * side : 1024 * (side + 1)].rearrange("p (r u e) -> p r u e", u=2, e=2)
            else:
                a_values = a_banks[s, side][:].bitcast(BF16).rearrange("p (u r e) -> p r u e", u=2, e=2)
            sigmoids = gate_values[2 * G + s // 2][:].rearrange("p u r e -> p r u e")
            h_words[s, G] = stage.tile([P, SLOTS * P], BF16, name="h_words", tag="h_words", align_bytes=64)
            nc.vector.tensor_tensor(
                out=h_words[s, G][:].rearrange("p (r u e) -> p r u e", u=2, e=2),
                in0=sigmoids[:, P * (s % 2) : P * (s % 2 + 1)],
                in1=a_values[:, P * k : P * (k + 1)],
                op=MULT,
            )

        def quantize_h(s, G):
            cols = slice(P * G, P * (G + 1))
            nc.vector.quantize_mx(
                out=h_codes[s][:, cols].bitcast(E4M3_X4), scales=h_code_scales[s][:, cols], in_=h_words[s, G][:]
            )

        def multiply_y(G, s, n):
            if G == 0:
                y[s, n] = bank(OUT_BANKS[s][n], "y")
            add_pass(y[s, n][:], G, s, 512 * n, 512)

        def add_pass(dst, G, s, lo, width):
            cols = slice(P * G, P * (G + 1))
            nc.tensor.matmul_mx(
                out=dst,
                lhsT=h_codes[s][:, cols].bitcast(E4M3_X4),
                lhsT_scale=h_code_scales[s][:, cols],
                rhs=wo_codes[G][:, 2 * lo : 2 * (lo + width)].bitcast(E2M1_X4),
                rhs_scale=wo_code_scales[:, G, lo : lo + width],
                start=(G == 0),
                stop=(G == NF - 1),
            )

        def store_y(src, s, lo, width, engine):
            if width == 512:
                y_rows = stage.tile([P, width], F32, name="y_rows", tag="w_wide", bufs=WIDE_BUFS, align_bytes=64)
            else:
                y_rows = stage.tile([P, width], F32, name="y_piece", tag="y_piece", bufs=len(LAST_PIECES), align_bytes=64)
            if engine is nc.scalar:
                nc.scalar.copy(out=y_rows[:], in_=src)
            else:
                nc.vector.tensor_copy(out=y_rows[:], in_=src)
            nc.sync.dma_start(out=out.rearrange("(p s) n -> s p n", s=NS)[s][:, lo : lo + width], in_=y_rows[:])

        with tc.manual_schedule():
            load_x_scale()
            nc.scalar.activation(out=warm[:, 1:2], in_=warm[:, 0:1], func=SIGMOID)
            load_x(0)
            load_x(1)
            row_halves = (slice(0, 2), slice(2, 4))
            load_w(0, row_halves[0])
            load_x(2)
            load_w(0, row_halves[1])
            load_x(3)
            load_wg_scale()
            for c in range(1, NC):
                load_w(c)
                for s in LOAD_A.get(c, ()):
                    load_a(s)
            load_wo_scales()
            for G in range(NF):
                load_wo(G)

            all_slots = slice(0, SLOTS)
            pair_slots = [slice(0, 2), slice(2, 4)]
            for s in range(NS):
                scale_x(s, nc.scalar)
                scale_x(s, nc.vector)
                turn_x(s)
                if s == 1:
                    for rows in row_halves:
                        widen(0, rows)
                    copy_x(0)
            widen(1)
            widen(2)
            copy_x(1)
            turn_a(2, 0)
            turn_a(2, 1)
            weave(0, all_slots, range(BLOCKS), nc.vector)
            quantize_x(0)
            weave(1, all_slots, (0, 1), nc.vector)
            quantize_w(0, 0, PASS)
            multiply_z(0, 0, 0)
            multiply_z(1, 0, 0)
            weave(1, all_slots, (2, 3), nc.vector)
            for c in range(NG, 1 + LEAD):
                widen(c)

            z_banks = [(pair, half) for half in range(2) for pair in range(2)]
            last = NC - 1
            for c in range(1, last - 1):
                G, g = divmod(c, NG)
                if g == 0:
                    for pair, half in z_banks if G < NF - 1 else z_banks[:-1]:
                        sigmoid(2 * (G - 1) + pair, half)
                for s, side in COPY_A.get(c, []):
                    copy_a(s, side)
                if c + LEAD < NC:
                    widen(c + LEAD)
                weave(c + 1, all_slots, (0, 1), nc.vector)
                quantize_w(G, PASS * g, PASS)
                if c == 1:
                    passes = [(pair, 1, 0) for pair in range(2)]
                    for pair, k, half in passes:
                        multiply_z(pair, k, half)
                    quantize_x(1)
                    passes = [(pair, k, 1) for pair in range(2) for k in range(2)]
                elif g == 0:
                    passes = [(pair, 0, half) for pair, half in z_banks[:-1]]
                elif g == 1:
                    passes = [(pair, 1, half) for pair, half in z_banks[:-1]] + [(1, 0, 1), (1, 1, 1)]
                else:
                    passes = [(pair, g, half) for pair, half in z_banks]
                for pair, k, half in passes:
                    multiply_z(2 * G + pair, k, half)
                for s, side in TURN_A.get(c, []):
                    turn_a(s, side)
                weave(c + 1, all_slots, (2, 3), nc.vector)

            gates = [(0, 0), (0, 1), (0, 2), (1, 0), (0, 3), (1, 1), (1, 2), (1, 3)]
            gates = gates + [(s, G) for s in (2, 3) for G in range(NF)]

            G, first, second = NF - 1, NQ - 2, NQ - 1
            weave(last, pair_slots[1], range(BLOCKS), nc.scalar)
            sigmoid(first - 1, 1)
            weave(last, pair_slots[0], (0, 1), nc.vector)
            quantize_w(G, PASS, PAIR)
            weave(last, pair_slots[0], (2, 3), nc.vector)
            quantize_w(G, PASS + PAIR, PAIR)
            quantize_w(G, 2 * PASS, PAIR)
            gate(*gates[0])
            quantize_w(G, 2 * PASS + PAIR, PAIR)
            for q, k, half in [(first, 1, 0), (first, 1, 1), (second, 1, 0), (first, 2, 0), (first, 2, 1)]:
                multiply_z(q, k, half)
            for k, half in [(0, 1), (1, 1), (2, 0), (2, 1)]:
                multiply_z(second, k, half)
            for q in (first, second):
                for half in range(2):
                    sigmoid(q, half)

            last_tile = NS - 1
            for i, (s, G) in enumerate(gates):
                if 0 < i < len(gates) - 1:
                    gate(*gates[i + 1])
                quantize_h(s, G)
                if i == 0:
                    gate(*gates[1])
                if s == last_tile or (s, G) == (last_tile - 1, NF - 2):
                    continue
                groups = (G - 1, G) if (s, G) == (last_tile - 1, NF - 1) else (G,)
                for n in range(NN):
                    for k in groups:
                        multiply_y(k, s, n)
                    if G == NF - 1:
                        store_y(y[s, n][:], s, 512 * n, 512, nc.scalar)

            for G in range(NF):
                multiply_y(G, last_tile, 0)
            store_y(y[last_tile, 0][:], last_tile, 0, 512, nc.scalar)
            lo = 512
            for k, (i, width) in enumerate(LAST_PIECES):
                piece = bank(i, "y")
                for G in range(NF):
                    add_pass(piece[:, :width], G, last_tile, lo, width)
                store_y(piece[:, :width], last_tile, lo, width, nc.scalar if k % 2 else nc.vector)
                lo = lo + width
